import numpy as np
import ml_dtypes


def mxq(x, axis, fmt="e4m3"):
    dtype, down = {"e4m3": (ml_dtypes.float8_e4m3fn, 7), "e5m2": (ml_dtypes.float8_e5m2, 14)}[fmt]
    v = np.moveaxis(np.asarray(x, np.float32).astype(ml_dtypes.bfloat16).astype(np.float64), axis, -1)
    blocks = v.reshape(v.shape[:-1] + (-1, 32))
    amax = np.abs(blocks).max(-1, keepdims=True)
    byte = np.maximum(np.where(amax > 0, np.frexp(amax)[1] - 1 + 127, 0) - down, 1)
    scale = np.exp2(byte - 127.0)
    codes = (blocks / scale).astype(np.float32).astype(dtype).astype(np.float64)
    return np.moveaxis((codes * scale).reshape(v.shape), -1, axis)


WIDE = False


def mx_kscale(k):
    if not WIDE:
        return np.ones(k)
    levels = np.array([10, -10, 5, -5, 0])
    if k % 512:
        return np.exp2(np.random.permutation(np.resize(levels, k // 32))).repeat(32)
    a = np.empty((k // 512, 16))
    for p in range(k // 512):
        a[p, :8] = np.random.permutation(np.resize(levels, 8))
        for g in range(8):
            far = levels[np.abs(levels - a[p, g]) >= 10]
            a[p, g + 8] = far[np.random.randint(len(far))]
    return np.exp2(a.ravel()).repeat(32)


def f64(x):
    return np.asarray(x).astype(np.float64)


def striped(idx):
    return np.tile(idx.reshape(-1, 16).T, (8, 1)).astype(np.uint16)


def unstriped(offs):
    return offs[:16].T.reshape(-1).astype(np.int64)


E2M1 = np.array([0.0, 0.5, 1.0, 1.5, 2.0, 3.0, 4.0, 6.0, -0.0, -0.5, -1.0, -1.5, -2.0, -3.0, -4.0, -6.0])


def pack_weight(w, fmt):
    k, n = w.shape
    w = f64(np.asarray(w, np.float32).astype(ml_dtypes.bfloat16)).reshape(k // 32, 32, n)
    amax = np.abs(w).max(1)
    if fmt == "e4m3":
        byte = np.frexp(amax)[1] - 1 + 127 - 7
    else:
        mant, ex = np.frexp(amax / 6.0)
        byte = np.where(mant > 0.5, ex, ex - 1) + 127
    byte = np.clip(np.where(amax > 0, byte, 1), 1, 254)
    scaled = (w * np.exp2(127.0 - byte)[:, None, :]).reshape(k, n).astype(np.float32)
    by_word = np.ascontiguousarray(scaled.reshape(k // 512, 128, 4, n).transpose(0, 1, 3, 2))
    if fmt == "e4m3":
        words = by_word.astype(ml_dtypes.float8_e4m3fn).view(np.uint8)
    else:
        c = by_word.astype(ml_dtypes.float4_e2m1fn).view(np.uint8) & 0xF
        words = (c[..., 0::2] | (c[..., 1::2] << 4)).reshape(k // 512, 128, 2 * n)
    return np.ascontiguousarray(words), np.ascontiguousarray(byte.astype(np.uint8).reshape(k // 512, 16, n))


def unpack_weight(words, scales, fmt):
    g, _, n = scales.shape
    words = np.ascontiguousarray(words).reshape(g, 128, n, -1)
    if fmt == "e4m3":
        vals = words.view(ml_dtypes.float8_e4m3fn).astype(np.float64)
    else:
        nib = np.empty((g, 128, n, 4), np.uint8)
        nib[..., 0::2] = words & 0xF
        nib[..., 1::2] = words >> 4
        vals = E2M1[nib]
    vals = vals * np.repeat(np.exp2(scales.astype(np.float64) - 127.0), 8, axis=1)[..., None]
    return vals.transpose(0, 1, 3, 2).reshape(g * 512, n)


def gelu(v):
    return 0.5 * v * (1.0 + np.tanh(np.sqrt(2.0 / np.pi) * (v + 0.044715 * v**3)))


K, T, S, H, N = 1024, 4096, 1024, 1024, 512

def setup_inputs():
    n = np.random.standard_normal
    s = mx_kscale(K)[:, None]
    u = mx_kscale(H)[:, None]
    tab_words, tab_scales = pack_weight(n((K, T)) * s, "e4m3")
    wk_words, wk_scales = pack_weight(n((K, H)) / np.sqrt(K) / s, "e2m1")
    return {
        "tab_words": tab_words, "tab_scales": tab_scales,
        "offs": striped(np.random.permutation(T)[:S]),
        "wk_words": wk_words, "wk_scales": wk_scales,
        "bk": (0.5 * n(H)).astype(np.float32),
        "wf": (n((K, H)) / np.sqrt(K) / s * u.T).astype(np.float32),
        "wm": (1.5 * n((H, N)) / np.sqrt(H) / u).astype(np.float32),
    }

def reference(tab_words, tab_scales, offs, wk_words, wk_scales, bk, wf, wm):
    v = unpack_weight(tab_words, tab_scales, "e4m3")[:, unstriped(offs)]
    wk = unpack_weight(wk_words, wk_scales, "e2m1")
    wfq = mxq(f64(wf), 0, "e4m3")
    wmq = mxq(f64(wm), 0, "e4m3")
    x = (wk.T @ v) + f64(bk)[:, None]
    g = 1.0 / (1.0 + x * x)
    f = wfq.T @ v
    h = mxq(f * g, 0, "e4m3")
    return wmq.T @ h

@@ -1,0 +1,252 @@
+from contextlib import ExitStack
+
+import concourse.mybir as mybir
+
+K, T, S, H, N = 1024, 4096, 1024, 1024, 512
+FLOPS = 2 * S * (K * H + K * H + H * N)
+
+F32 = mybir.dt.float32
+BF16 = mybir.dt.bfloat16
+I32 = mybir.dt.int32
+U32 = mybir.dt.uint32
+U16 = mybir.dt.uint16
+U8 = mybir.dt.uint8
+FP8X4 = mybir.dt.float8_e4m3fn_x4
+FP4X4 = mybir.dt.float4_e2m1fn_x4
+ACT = mybir.ActivationFunctionType
+MULT = mybir.AluOpType.mult
+
+P = 128
+PACK = 4
+PASS = P * PACK
+HALF = 512
+CHUNK = 128
+
+
+def tile_list_ball_cauchy_mix_kernel(tc, tab_words, tab_scales, offs, wk_words, wk_scales, bk, wf, wm, out):
+    nc = tc.nc
+    with ExitStack() as ctx:
+        keep = ctx.enter_context(tc.tile_pool(name="keep", bufs=1))
+        cast = ctx.enter_context(tc.tile_pool(name="cast", bufs=3))
+        hpool = ctx.enter_context(tc.tile_pool(name="hpool", bufs=3))
+        opool = ctx.enter_context(tc.tile_pool(name="opool", bufs=3))
+        xps = ctx.enter_context(tc.psum_pool(name="xps", bufs=2))
+        fps = ctx.enter_context(tc.psum_pool(name="fps", bufs=3))
+        ops = ctx.enter_context(tc.psum_pool(name="ops", bufs=3))
+
+        offsets = keep.tile([P, S // 16], U16, name="offsets")
+        nc.sync.dma_start(offsets[:], offs)
+
+        tscale = keep.tile([P, T // 4], I32, name="tscale", align_bytes=64)
+        nc.sync.dma_start(tscale[0:32, :], tab_scales.rearrange("a q c -> (a q) c").bitcast(I32))
+        kscale_raw = keep.tile([P, H // 4], I32, name="kscale_raw", align_bytes=64)
+        nc.sync.dma_start(kscale_raw[0:32, :], wk_scales.rearrange("a q c -> (a q) c").bitcast(I32))
+
+        wk_view = wk_words.rearrange("a p c -> p a c")
+        wkp = [keep.tile([P, 2, PASS // 2], I32, name="wkp%d" % b, align_bytes=64) for b in range(2)]
+
+        def load_wk(b):
+            raw = keep.tile([P, 2, PASS // 2], I32, name="wk_raw", tag="wk_raw", align_bytes=64)
+            nc.sync.dma_start(raw[:], wk_view[:, :, 2 * PASS * b : 2 * PASS * (b + 1)].bitcast(I32))
+            return raw
+
+        def permute_wk(b, raw):
+            nc.vector.tensor_copy(
+                out=wkp[b][:].bitcast(U16).rearrange("p a (t m) -> p a m t", t=PACK),
+                in_=raw[:].bitcast(U16).rearrange("p a (m t) -> p a m t", t=PACK),
+            )
+
+        wk_raw0 = load_wk(0)
+        table = [keep.tile([P, T], I32, name="table%d" % a, align_bytes=64) for a in range(2)]
+        for a in range(2):
+            nc.sync.dma_start(table[a][:], tab_words[a].rearrange("p n t -> p (n t)").bitcast(I32))
+
+        nc.vector.memset(tscale[32:64, :], 0)
+        nc.vector.memset(tscale[64:128, :], 0)
+        nc.vector.memset(kscale_raw[32:64, :], 0)
+        nc.vector.memset(kscale_raw[64:128, :], 0)
+        planes = keep.tile([P, 2, (S + H) // 4], I32, name="planes", align_bytes=64)
+        nc.vector.memset(planes[:], 0)
+
+        picked = keep.tile([P, S // 4], I32, name="picked", align_bytes=64)
+        nc.vector.tensor_copy(picked[:].bitcast(U8), tscale[:].bitcast(U8).indirect(offsets[:]))
+        rows = keep.tile([P, (S + H) // 4], I32, name="rows", tag="stage", align_bytes=64)
+        nc.vector.tensor_copy(
+            out=rows[:, S // 4 :].bitcast(U8).rearrange("p (b t m) -> p b m t", b=2, t=PACK),
+            in_=kscale_raw[:].bitcast(U8).rearrange("p (b m t) -> p b m t", b=2, t=PACK),
+        )
+        nc.vector.tensor_copy(rows[0:32, 0 : S // 4], picked[0:32, :])
+        permute_wk(0, wk_raw0)
+        wk_raw1 = load_wk(1)
+        for a in range(2):
+            for q in range(4):
+                eng = nc.gpsimd if q == 0 else nc.scalar
+                eng.dma_start(planes[32 * q : 32 * q + 4, a, :], rows[16 * a + 4 * q : 16 * a + 4 * q + 4, :])
+
+        stage = keep.tile([P, 6 * PACK * HALF + 16], F32, name="stage", tag="stage", align_bytes=64)
+        bias = stage[:, 6 * PACK * HALF : 6 * PACK * HALF + 8]
+        nc.sync.dma_start(bias.rearrange("p (b t) -> p b t", b=2), bk.rearrange("(b p t) -> p b t", b=2, t=PACK))
+
+        def raw_slot(i):
+            return stage[:, i * PACK * HALF : (i + 1) * PACK * HALF].rearrange("p (j c) -> p j c", j=PACK)
+
+        for b in range(2):
+            for a in range(2):
+                src = wf[a * PASS : (a + 1) * PASS, b * PASS : (b + 1) * PASS]
+                nc.sync.dma_start(raw_slot(2 * b + a), src.rearrange("(p j) c -> p j c", j=PACK))
+        for b in range(2):
+            nc.sync.dma_start(raw_slot(4 + b), wm[b * PASS : (b + 1) * PASS, :].rearrange("(p j) c -> p j c", j=PACK))
+
+        vw = [keep.tile([P, S], I32, name="vw%d" % a, align_bytes=64) for a in range(2)]
+        nc.vector.tensor_copy(vw[0][:].bitcast(U32), table[0][:].bitcast(U32).indirect(offsets[:]))
+        for h in range(2):
+            nc.vector.tensor_copy(
+                vw[1][:, h * HALF : (h + 1) * HALF].bitcast(U32),
+                table[1][:].bitcast(U32).indirect(offsets[:, h * HALF // 16 : (h + 1) * HALF // 16]),
+            )
+        planes8 = planes[:].bitcast(U8)
+
+        wfq = {}
+        wmq = {}
+
+        def quant_wf(a, b):
+            g = cast.tile([P, PACK * PASS], BF16, name="grouped", tag="grouped", align_bytes=64)
+            nc.vector.tensor_copy(
+                out=g[:].rearrange("p (t m j) -> p m j t", t=PACK, j=PACK),
+                in_=raw_slot(2 * b + a).rearrange("p j (m t) -> p m j t", t=PACK),
+            )
+            codes = keep.tile([P, PASS], U32, name="wfc%d%d" % (a, b), align_bytes=64)
+            scales = keep.tile([P, PASS], U8, name="wfs%d%d" % (a, b), align_bytes=64)
+            nc.vector.quantize_mx(out=codes[:].bitcast(FP8X4), scales=scales[:], in_=g[:])
+            wfq[a, b] = (codes, scales)
+
+        def quant_wm(b):
+            g = cast.tile([P, PACK * N], BF16, name="grouped", tag="grouped", align_bytes=64)
+            nc.vector.tensor_copy(
+                out=g[:].rearrange("p (c i j) -> p c j i", i=4, j=PACK),
+                in_=raw_slot(4 + b).rearrange("p j (c i) -> p c j i", i=4),
+            )
+            codes = keep.tile([P, N], U32, name="wmc%d" % b, align_bytes=64)
+            scales = keep.tile([P, N], U8, name="wms%d" % b, align_bytes=64)
+            nc.vector.quantize_mx(out=codes[:].bitcast(FP8X4), scales=scales[:], in_=g[:])
+            wmq[b] = (codes, scales)
+
+        ys = {}
+
+        def squares(b, h):
+            y = keep.tile([P, HALF // CHUNK, PACK, CHUNK], F32, name="y%d%d" % (b, h))
+            ys[b, h] = y
+            tok = slice(h * HALF, (h + 1) * HALF)
+            for t in range(PACK):
+                x = xps.tile([P, HALF], F32, name="x")
+                for a in range(2):
+                    c0 = S + b * PASS + t * P
+                    nc.tensor.matmul_mx(
+                        out=x[:],
+                        lhsT=wkp[b][:, a, t * P // 2 : (t + 1) * P // 2].bitcast(U8).bitcast(FP4X4),
+                        lhsT_scale=planes8[:, a, c0 : c0 + P],
+                        rhs=vw[a][:, tok].bitcast(FP8X4),
+                        rhs_scale=planes8[:, a, tok],
+                        start=(a == 0),
+                        stop=(a == 1),
+                    )
+                nc.scalar.activation(
+                    out=y[:, :, t, :],
+                    in_=x[:].rearrange("p (c n) -> p c n", n=CHUNK),
+                    func=ACT.Square,
+                    bias=bias[:, PACK * b + t : PACK * b + t + 1],
+                )
+
+        def cauchy(b, h, c0, c1):
+            part = ys[b, h][:, c0:c1, :, :].rearrange("p c t n -> p (c t n)")
+            nc.scalar.activation(out=part, in_=part, func=ACT.Abs_reciprocal_sqrt, bias=1.0)
+            nc.scalar.activation(out=part, in_=part, func=ACT.Square)
+
+        hc = [keep.tile([P, S], U32, name="hc%d" % b, align_bytes=64) for b in range(2)]
+        hs = [keep.tile([P, S], U8, name="hs%d" % b, align_bytes=64) for b in range(2)]
+
+        def hidden(b, h, c0, c1):
+            hb = hpool.tile([P, c1 - c0, CHUNK * PACK], BF16, name="hb", tag="hb", align_bytes=64)
+            for c in range(c0, c1):
+                tok = slice(h * HALF + c * CHUNK, h * HALF + (c + 1) * CHUNK)
+                f = fps.tile([P, PACK, CHUNK], F32, name="f")
+                for t in range(PACK):
+                    for a in range(2):
+                        codes, scales = wfq[a, b]
+                        nc.tensor.matmul_mx(
+                            out=f[:, t, :],
+                            lhsT=codes[:, t * P : (t + 1) * P].bitcast(FP8X4),
+                            lhsT_scale=scales[:, t * P : (t + 1) * P],
+                            rhs=vw[a][:, tok].bitcast(FP8X4),
+                            rhs_scale=planes8[:, a, tok],
+                            start=(a == 0),
+                            stop=(a == 1),
+                        )
+                nc.vector.tensor_tensor(
+                    out=hb[:, c - c0, :].rearrange("p (u i t) -> p u t i", i=4, t=PACK),
+                    in0=f[:].rearrange("p t (u i) -> p u t i", i=4),
+                    in1=ys[b, h][:, c, :, :].rearrange("p t (u i) -> p u t i", i=4),
+                    op=MULT,
+                )
+            tok = slice(h * HALF + c0 * CHUNK, h * HALF + c1 * CHUNK)
+            nc.vector.quantize_mx(
+                out=hc[b][:, tok].bitcast(FP8X4), scales=hs[b][:, tok], in_=hb[:].rearrange("p c w -> p (c w)")
+            )
+
+        out_view = out.rearrange("(g p) s -> p g s", p=P)
+
+        def mix(h, c0, c1, engines):
+            width = (c1 - c0) * CHUNK
+            tok = slice(h * HALF + c0 * CHUNK, h * HALF + c1 * CHUNK)
+            per_bank = HALF // width
+            res = opool.tile([P, N // P, width], F32, name="res", tag="res")
+            for g0 in range(0, N // P, per_bank):
+                acc = ops.tile([P, per_bank, width], F32, name="acc", tag="acc")
+                for g in range(g0, g0 + per_bank):
+                    for b in range(2):
+                        codes, scales = wmq[b]
+                        nc.tensor.matmul_mx(
+                            out=acc[:, g - g0, :],
+                            lhsT=codes[:, g * P : (g + 1) * P].bitcast(FP8X4),
+                            lhsT_scale=scales[:, g * P : (g + 1) * P],
+                            rhs=hc[b][:, tok].bitcast(FP8X4),
+                            rhs_scale=hs[b][:, tok],
+                            start=(b == 0),
+                            stop=(b == 1),
+                        )
+                if engines[g0 // per_bank] == "v":
+                    nc.vector.tensor_copy(out=res[:, g0 : g0 + per_bank, :], in_=acc[:])
+                else:
+                    nc.scalar.copy(out=res[:, g0 : g0 + per_bank, :], in_=acc[:])
+            nc.sync.dma_start(out_view[:, :, tok], res[:])
+
+        squares(0, 0)
+        quant_wf(0, 0)
+        permute_wk(1, wk_raw1)
+        quant_wf(1, 0)
+        for c in range(0, 4, 2):
+            cauchy(0, 0, c, c + 2)
+            hidden(0, 0, c, c + 2)
+        squares(1, 0)
+        squares(0, 1)
+        squares(1, 1)
+        quant_wf(0, 1)
+        quant_wf(1, 1)
+        quant_wm(0)
+        quant_wm(1)
+        for c in range(0, 4, 2):
+            cauchy(1, 0, c, c + 2)
+            hidden(1, 0, c, c + 2)
+            mix(0, c, c + 2, "vv")
+        for c in range(0, 4, 2):
+            cauchy(0, 1, c, c + 2)
+            hidden(0, 1, c, c + 2)
+        cauchy(1, 1, 0, 2)
+        hidden(1, 1, 0, 2)
+        mix(1, 0, 2, "vv")
+        cauchy(1, 1, 2, 3)
+        hidden(1, 1, 2, 3)
+        cauchy(1, 1, 3, 4)
+        hidden(1, 1, 3, 4)
+        mix(1, 2, 3, "s")
+        mix(1, 3, 4, "s")

@@ -27,12 +27,13 @@ def tile_list_ball_cauchy_mix_kernel(tc, tab_words, tab_scales, offs, wk_words, 
     nc = tc.nc
     with ExitStack() as ctx:
         keep = ctx.enter_context(tc.tile_pool(name="keep", bufs=1))
+        stage = ctx.enter_context(tc.tile_pool(name="stage", bufs=1))
         cast = ctx.enter_context(tc.tile_pool(name="cast", bufs=3))
         hpool = ctx.enter_context(tc.tile_pool(name="hpool", bufs=3))
         opool = ctx.enter_context(tc.tile_pool(name="opool", bufs=3))
-        xps = ctx.enter_context(tc.psum_pool(name="xps", bufs=2))
+        xps = ctx.enter_context(tc.psum_pool(name="xps", bufs=3))
         fps = ctx.enter_context(tc.psum_pool(name="fps", bufs=3))
-        ops = ctx.enter_context(tc.psum_pool(name="ops", bufs=3))
+        ops = ctx.enter_context(tc.psum_pool(name="ops", bufs=2))
 
         offsets = keep.tile([P, S // 16], U16, name="offsets")
         nc.sync.dma_start(offsets[:], offs)
@@ -41,6 +42,10 @@ def tile_list_ball_cauchy_mix_kernel(tc, tab_words, tab_scales, offs, wk_words, 
         nc.sync.dma_start(tscale[0:32, :], tab_scales.rearrange("a q c -> (a q) c").bitcast(I32))
         kscale_raw = keep.tile([P, H // 4], I32, name="kscale_raw", align_bytes=64)
         nc.sync.dma_start(kscale_raw[0:32, :], wk_scales.rearrange("a q c -> (a q) c").bitcast(I32))
+
+        warm = keep.tile([P, 2], F32, name="warm")
+        nc.gpsimd.memset(warm[:, 0:1], 1.0)
+        nc.scalar.activation(out=warm[:, 1:2], in_=warm[:, 0:1], func=ACT.Abs_reciprocal_sqrt)
 
         wk_view = wk_words.rearrange("a p c -> p a c")
         wkp = [keep.tile([P, 2, PASS // 2], I32, name="wkp%d" % b, align_bytes=64) for b in range(2)]
@@ -52,8 +57,8 @@ def tile_list_ball_cauchy_mix_kernel(tc, tab_words, tab_scales, offs, wk_words, 
 
         def permute_wk(b, raw):
             nc.vector.tensor_copy(
-                out=wkp[b][:].bitcast(U16).rearrange("p a (t m) -> p a m t", t=PACK),
-                in_=raw[:].bitcast(U16).rearrange("p a (m t) -> p a m t", t=PACK),
+                out=wkp[b][:].rearrange("p a (t v w) -> p a v t w", t=PACK, w=4),
+                in_=raw.rearrange("p a (v w t) -> p a v t w", t=PACK, w=4),
             )
 
         wk_raw0 = load_wk(0)
@@ -70,32 +75,39 @@ def tile_list_ball_cauchy_mix_kernel(tc, tab_words, tab_scales, offs, wk_words, 
 
         picked = keep.tile([P, S // 4], I32, name="picked", align_bytes=64)
         nc.vector.tensor_copy(picked[:].bitcast(U8), tscale[:].bitcast(U8).indirect(offsets[:]))
-        rows = keep.tile([P, (S + H) // 4], I32, name="rows", tag="stage", align_bytes=64)
+        region = stage.tile([P, 6 * PACK * HALF + 16 + PASS], I32, name="region", align_bytes=64, offset=0)
+        rows = region[:, 0 : (S + H) // 4]
         nc.vector.tensor_copy(
-            out=rows[:, S // 4 :].bitcast(U8).rearrange("p (b t m) -> p b m t", b=2, t=PACK),
-            in_=kscale_raw[:].bitcast(U8).rearrange("p (b m t) -> p b m t", b=2, t=PACK),
+            out=rows[:, S // 4 :].bitcast(U16).rearrange("p (b t u) -> p b t u", b=2, t=PACK),
+            in_=kscale_raw[:].bitcast(U16).rearrange("p (b u t) -> p b t u", b=2, t=PACK),
         )
         nc.vector.tensor_copy(rows[0:32, 0 : S // 4], picked[0:32, :])
-        permute_wk(0, wk_raw0)
-        wk_raw1 = load_wk(1)
-        for a in range(2):
-            for q in range(4):
-                eng = nc.gpsimd if q == 0 else nc.scalar
-                eng.dma_start(planes[32 * q : 32 * q + 4, a, :], rows[16 * a + 4 * q : 16 * a + 4 * q + 4, :])
+        permute_wk(0, wk_raw0[:])
+        nc.vector.tensor_copy(planes[0:32, 0, :], rows[0:32, :])
+        for row in range(4, 32, 4):
+            a, q = divmod(row // 4, 4)
+            nc.scalar.dma_start(planes[32 * q : 32 * q + 4, a, :], rows[row : row + 4, :])
 
-        stage = keep.tile([P, 6 * PACK * HALF + 16], F32, name="stage", tag="stage", align_bytes=64)
-        bias = stage[:, 6 * PACK * HALF : 6 * PACK * HALF + 8]
-        nc.sync.dma_start(bias.rearrange("p (b t) -> p b t", b=2), bk.rearrange("(b p t) -> p b t", b=2, t=PACK))
+        slot = 4 * PACK * HALF
+        bias = stage.tile([P, 2, 8], F32, name="bias", align_bytes=64, offset=6 * slot)
+        for e in range(2):
+            nc.sync.dma_start(bias[e:P:2, :, 0:7], bk.rearrange("(b u k) -> u b k", b=2, k=8)[:, :, e : e + 7])
+        wk_late = stage.tile([P, 2, PASS // 2], I32, name="wk_late", align_bytes=64, offset=6 * slot + 64)
+        wk_raw1 = wk_late[:]
+        raws = [stage.tile([P, PACK, HALF], F32, name="raw%d" % i, align_bytes=64, offset=i * slot) for i in range(6)]
+        nc.sync.dma_start(wk_raw1, wk_view[:, :, 2 * PASS : 4 * PASS].bitcast(I32))
 
         def raw_slot(i):
-            return stage[:, i * PACK * HALF : (i + 1) * PACK * HALF].rearrange("p (j c) -> p j c", j=PACK)
+            return raws[i][:]
 
         for b in range(2):
             for a in range(2):
                 src = wf[a * PASS : (a + 1) * PASS, b * PASS : (b + 1) * PASS]
                 nc.sync.dma_start(raw_slot(2 * b + a), src.rearrange("(p j) c -> p j c", j=PACK))
         for b in range(2):
-            nc.sync.dma_start(raw_slot(4 + b), wm[b * PASS : (b + 1) * PASS, :].rearrange("(p j) c -> p j c", j=PACK))
+            src = wm[b * PASS : (b + 1) * PASS, :].rearrange("(u t e) c -> e u t c", t=PACK, e=2)
+            for e in range(2):
+                nc.sync.dma_start(raw_slot(4 + b)[e:P:2], src[e])
 
         vw = [keep.tile([P, S], I32, name="vw%d" % a, align_bytes=64) for a in range(2)]
         nc.vector.tensor_copy(vw[0][:].bitcast(U32), table[0][:].bitcast(U32).indirect(offsets[:]))
@@ -112,8 +124,8 @@ def tile_list_ball_cauchy_mix_kernel(tc, tab_words, tab_scales, offs, wk_words, 
         def quant_wf(a, b):
             g = cast.tile([P, PACK * PASS], BF16, name="grouped", tag="grouped", align_bytes=64)
             nc.vector.tensor_copy(
-                out=g[:].rearrange("p (t m j) -> p m j t", t=PACK, j=PACK),
-                in_=raw_slot(2 * b + a).rearrange("p j (m t) -> p m j t", t=PACK),
+                out=g[:].rearrange("p (t u e j) -> p t u j e", t=PACK, e=2, j=PACK),
+                in_=raw_slot(2 * b + a).rearrange("p j (u t e) -> p t u j e", t=PACK, e=2),
             )
             codes = keep.tile([P, PASS], U32, name="wfc%d%d" % (a, b), align_bytes=64)
             scales = keep.tile([P, PASS], U8, name="wfs%d%d" % (a, b), align_bytes=64)
@@ -123,21 +135,24 @@ def tile_list_ball_cauchy_mix_kernel(tc, tab_words, tab_scales, offs, wk_words, 
         def quant_wm(b):
             g = cast.tile([P, PACK * N], BF16, name="grouped", tag="grouped", align_bytes=64)
             nc.vector.tensor_copy(
-                out=g[:].rearrange("p (c i j) -> p c j i", i=4, j=PACK),
-                in_=raw_slot(4 + b).rearrange("p j (c i) -> p c j i", i=4),
+                out=g[:].rearrange("p (c i j) -> p c j i", i=2, j=PACK),
+                in_=raw_slot(4 + b).rearrange("p j (c i) -> p c j i", i=2),
             )
             codes = keep.tile([P, N], U32, name="wmc%d" % b, align_bytes=64)
             scales = keep.tile([P, N], U8, name="wms%d" % b, align_bytes=64)
             nc.vector.quantize_mx(out=codes[:].bitcast(FP8X4), scales=scales[:], in_=g[:])
             wmq[b] = (codes, scales)
 
-        ys = {}
+        ys = {
+            (b, h): keep.tile([P, HALF // CHUNK, PACK, CHUNK], F32, name="y%d%d" % (b, h))
+            for b in range(2)
+            for h in range(2)
+        }
 
-        def squares(b, h):
-            y = keep.tile([P, HALF // CHUNK, PACK, CHUNK], F32, name="y%d%d" % (b, h))
-            ys[b, h] = y
+        def squares(b, h, slots):
+            y = ys[b, h]
             tok = slice(h * HALF, (h + 1) * HALF)
-            for t in range(PACK):
+            for t in slots:
                 x = xps.tile([P, HALF], F32, name="x")
                 for a in range(2):
                     c0 = S + b * PASS + t * P
@@ -154,13 +169,18 @@ def tile_list_ball_cauchy_mix_kernel(tc, tab_words, tab_scales, offs, wk_words, 
                     out=y[:, :, t, :],
                     in_=x[:].rearrange("p (c n) -> p c n", n=CHUNK),
                     func=ACT.Square,
-                    bias=bias[:, PACK * b + t : PACK * b + t + 1],
+                    bias=bias[:, b, 2 * t : 2 * t + 1],
                 )
 
-        def cauchy(b, h, c0, c1):
+        def cauchy(b, h, c0, c1, eng):
             part = ys[b, h][:, c0:c1, :, :].rearrange("p c t n -> p (c t n)")
             nc.scalar.activation(out=part, in_=part, func=ACT.Abs_reciprocal_sqrt, bias=1.0)
-            nc.scalar.activation(out=part, in_=part, func=ACT.Square)
+            if eng == "S":
+                nc.scalar.activation(out=part, in_=part, func=ACT.Square)
+            elif eng == "V":
+                nc.vector.tensor_tensor(out=part, in0=part, in1=part, op=MULT)
+            else:
+                nc.gpsimd.tensor_tensor(out=part, in0=part, in1=part, op=MULT)
 
         hc = [keep.tile([P, S], U32, name="hc%d" % b, align_bytes=64) for b in range(2)]
         hs = [keep.tile([P, S], U8, name="hs%d" % b, align_bytes=64) for b in range(2)]
@@ -183,9 +203,9 @@ def tile_list_ball_cauchy_mix_kernel(tc, tab_words, tab_scales, offs, wk_words, 
                             stop=(a == 1),
                         )
                 nc.vector.tensor_tensor(
-                    out=hb[:, c - c0, :].rearrange("p (u i t) -> p u t i", i=4, t=PACK),
-                    in0=f[:].rearrange("p t (u i) -> p u t i", i=4),
-                    in1=ys[b, h][:, c, :, :].rearrange("p t (u i) -> p u t i", i=4),
+                    out=hb[:, c - c0, :].rearrange("p (u i t) -> p u t i", i=2, t=PACK),
+                    in0=f[:].rearrange("p t (u i) -> p u t i", i=2),
+                    in1=ys[b, h][:, c, :, :].rearrange("p t (u i) -> p u t i", i=2),
                     op=MULT,
                 )
             tok = slice(h * HALF + c0 * CHUNK, h * HALF + c1 * CHUNK)
@@ -220,33 +240,41 @@ def tile_list_ball_cauchy_mix_kernel(tc, tab_words, tab_scales, offs, wk_words, 
                     nc.scalar.copy(out=res[:, g0 : g0 + per_bank, :], in_=acc[:])
             nc.sync.dma_start(out_view[:, :, tok], res[:])
 
-        squares(0, 0)
-        quant_wf(0, 0)
         permute_wk(1, wk_raw1)
+        squares(0, 0, (0, 1,))
+        squares(0, 0, (2, 3,))
+        cauchy(0, 0, 0, 2, "S")
+        squares(1, 0, (2, 3,))
+        squares(0, 1, (0, 1,))
+        cauchy(0, 0, 2, 4, "S")
+        squares(1, 1, (0, 1,))
+        squares(1, 0, (0, 1,))
+        quant_wf(0, 0)
         quant_wf(1, 0)
-        for c in range(0, 4, 2):
-            cauchy(0, 0, c, c + 2)
-            hidden(0, 0, c, c + 2)
-        squares(1, 0)
-        squares(0, 1)
-        squares(1, 1)
+        hidden(0, 0, 0, 2)
+        squares(0, 1, (2, 3,))
         quant_wf(0, 1)
         quant_wf(1, 1)
         quant_wm(0)
+        cauchy(1, 0, 0, 2, "S")
+        cauchy(1, 0, 2, 4, "V")
+        cauchy(0, 1, 0, 2, "S")
+        hidden(0, 0, 2, 4)
+        squares(1, 1, (2, 3,))
+        hidden(1, 0, 0, 2)
         quant_wm(1)
-        for c in range(0, 4, 2):
-            cauchy(1, 0, c, c + 2)
-            hidden(1, 0, c, c + 2)
-            mix(0, c, c + 2, "vv")
-        for c in range(0, 4, 2):
-            cauchy(0, 1, c, c + 2)
-            hidden(0, 1, c, c + 2)
-        cauchy(1, 1, 0, 2)
+        hidden(1, 0, 2, 4)
+        cauchy(0, 1, 2, 4, "S")
+        hidden(0, 1, 0, 2)
+        hidden(0, 1, 2, 4)
+        mix(0, 0, 2, "vs")
+        cauchy(1, 1, 0, 2, "S")
+        cauchy(1, 1, 2, 3, "S")
         hidden(1, 1, 0, 2)
-        mix(1, 0, 2, "vv")
-        cauchy(1, 1, 2, 3)
+        mix(0, 2, 4, "sv")
+        mix(1, 0, 2, "ss")
         hidden(1, 1, 2, 3)
-        cauchy(1, 1, 3, 4)
+        mix(1, 2, 3, "v")
+        cauchy(1, 1, 3, 4, "S")
         hidden(1, 1, 3, 4)
-        mix(1, 2, 3, "s")
-        mix(1, 3, 4, "s")
+        mix(1, 3, 4, "v")

@@ -30,10 +30,10 @@ def tile_list_ball_cauchy_mix_kernel(tc, tab_words, tab_scales, offs, wk_words, 
         stage = ctx.enter_context(tc.tile_pool(name="stage", bufs=1))
         cast = ctx.enter_context(tc.tile_pool(name="cast", bufs=3))
         hpool = ctx.enter_context(tc.tile_pool(name="hpool", bufs=3))
-        opool = ctx.enter_context(tc.tile_pool(name="opool", bufs=3))
-        xps = ctx.enter_context(tc.psum_pool(name="xps", bufs=3))
+        opool = ctx.enter_context(tc.tile_pool(name="opool", bufs=6))
+        xps = ctx.enter_context(tc.psum_pool(name="xps", bufs=2))
         fps = ctx.enter_context(tc.psum_pool(name="fps", bufs=3))
-        ops = ctx.enter_context(tc.psum_pool(name="ops", bufs=2))
+        ops = ctx.enter_context(tc.psum_pool(name="ops", bufs=3))
 
         offsets = keep.tile([P, S // 16], U16, name="offsets")
         nc.sync.dma_start(offsets[:], offs)
@@ -46,6 +46,10 @@ def tile_list_ball_cauchy_mix_kernel(tc, tab_words, tab_scales, offs, wk_words, 
         warm = keep.tile([P, 2], F32, name="warm")
         nc.gpsimd.memset(warm[:, 0:1], 1.0)
         nc.scalar.activation(out=warm[:, 1:2], in_=warm[:, 0:1], func=ACT.Abs_reciprocal_sqrt)
+
+        bias = keep.tile([P, 2, 8], F32, name="bias", align_bytes=64)
+        for e in range(2):
+            nc.gpsimd.dma_start(bias[e:P:2, :, 0:7], bk.rearrange("(b u k) -> u b k", b=2, k=8)[:, :, e : e + 7])
 
         wk_view = wk_words.rearrange("a p c -> p a c")
         wkp = [keep.tile([P, 2, PASS // 2], I32, name="wkp%d" % b, align_bytes=64) for b in range(2)]
@@ -75,7 +79,7 @@ def tile_list_ball_cauchy_mix_kernel(tc, tab_words, tab_scales, offs, wk_words, 
 
         picked = keep.tile([P, S // 4], I32, name="picked", align_bytes=64)
         nc.vector.tensor_copy(picked[:].bitcast(U8), tscale[:].bitcast(U8).indirect(offsets[:]))
-        region = stage.tile([P, 6 * PACK * HALF + 16 + PASS], I32, name="region", align_bytes=64, offset=0)
+        region = stage.tile([P, 6 * PACK * HALF + PASS], I32, name="region", align_bytes=64, offset=0)
         rows = region[:, 0 : (S + H) // 4]
         nc.vector.tensor_copy(
             out=rows[:, S // 4 :].bitcast(U16).rearrange("p (b t u) -> p b t u", b=2, t=PACK),
@@ -86,16 +90,13 @@ def tile_list_ball_cauchy_mix_kernel(tc, tab_words, tab_scales, offs, wk_words, 
         nc.vector.tensor_copy(planes[0:32, 0, :], rows[0:32, :])
         for row in range(4, 32, 4):
             a, q = divmod(row // 4, 4)
-            nc.scalar.dma_start(planes[32 * q : 32 * q + 4, a, :], rows[row : row + 4, :])
+            queue = nc.gpsimd if row == 4 else nc.scalar
+            queue.dma_start(planes[32 * q : 32 * q + 4, a, :], rows[row : row + 4, :])
 
         slot = 4 * PACK * HALF
-        bias = stage.tile([P, 2, 8], F32, name="bias", align_bytes=64, offset=6 * slot)
-        for e in range(2):
-            nc.sync.dma_start(bias[e:P:2, :, 0:7], bk.rearrange("(b u k) -> u b k", b=2, k=8)[:, :, e : e + 7])
-        wk_late = stage.tile([P, 2, PASS // 2], I32, name="wk_late", align_bytes=64, offset=6 * slot + 64)
+        wk_late = stage.tile([P, 2, PASS // 2], I32, name="wk_late", align_bytes=64, offset=6 * slot)
         wk_raw1 = wk_late[:]
         raws = [stage.tile([P, PACK, HALF], F32, name="raw%d" % i, align_bytes=64, offset=i * slot) for i in range(6)]
-        nc.sync.dma_start(wk_raw1, wk_view[:, :, 2 * PASS : 4 * PASS].bitcast(I32))
 
         def raw_slot(i):
             return raws[i][:]
@@ -104,6 +105,8 @@ def tile_list_ball_cauchy_mix_kernel(tc, tab_words, tab_scales, offs, wk_words, 
             for a in range(2):
                 src = wf[a * PASS : (a + 1) * PASS, b * PASS : (b + 1) * PASS]
                 nc.sync.dma_start(raw_slot(2 * b + a), src.rearrange("(p j) c -> p j c", j=PACK))
+                if (a, b) == (0, 0):
+                    nc.sync.dma_start(wk_raw1, wk_view[:, :, 2 * PASS : 4 * PASS].bitcast(I32))
         for b in range(2):
             src = wm[b * PASS : (b + 1) * PASS, :].rearrange("(u t e) c -> e u t c", t=PACK, e=2)
             for e in range(2):
@@ -153,7 +156,10 @@ def tile_list_ball_cauchy_mix_kernel(tc, tab_words, tab_scales, offs, wk_words, 
             y = ys[b, h]
             tok = slice(h * HALF, (h + 1) * HALF)
             for t in slots:
-                x = xps.tile([P, HALF], F32, name="x")
+                if (b, h) == (0, 0) and t >= 2:
+                    x = ops.tile([P, HALF], F32, name="acc", tag="acc")
+                else:
+                    x = xps.tile([P, HALF], F32, name="x", tag="x")
                 for a in range(2):
                     c0 = S + b * PASS + t * P
                     nc.tensor.matmul_mx(
@@ -218,10 +224,15 @@ def tile_list_ball_cauchy_mix_kernel(tc, tab_words, tab_scales, offs, wk_words, 
         def mix(h, c0, c1, engines):
             width = (c1 - c0) * CHUNK
             tok = slice(h * HALF + c0 * CHUNK, h * HALF + c1 * CHUNK)
-            per_bank = HALF // width
-            res = opool.tile([P, N // P, width], F32, name="res", tag="res")
+            per_bank = (N // P) // len(engines)
+            per_store = max(per_bank, 2)
             for g0 in range(0, N // P, per_bank):
-                acc = ops.tile([P, per_bank, width], F32, name="acc", tag="acc")
+                if g0 % per_store == 0:
+                    res = opool.tile([P, per_store, width], F32, name="res", tag="res")
+                if per_bank == 1 and g0 % 2 == 1:
+                    acc = xps.tile([P, per_bank, width], F32, name="x", tag="x")
+                else:
+                    acc = ops.tile([P, per_bank, width], F32, name="acc", tag="acc")
                 for g in range(g0, g0 + per_bank):
                     for b in range(2):
                         codes, scales = wmq[b]
@@ -234,47 +245,49 @@ def tile_list_ball_cauchy_mix_kernel(tc, tab_words, tab_scales, offs, wk_words, 
                             start=(b == 0),
                             stop=(b == 1),
                         )
+                r0 = g0 % per_store
                 if engines[g0 // per_bank] == "v":
-                    nc.vector.tensor_copy(out=res[:, g0 : g0 + per_bank, :], in_=acc[:])
+                    nc.vector.tensor_copy(out=res[:, r0 : r0 + per_bank, :], in_=acc[:])
                 else:
-                    nc.scalar.copy(out=res[:, g0 : g0 + per_bank, :], in_=acc[:])
-            nc.sync.dma_start(out_view[:, :, tok], res[:])
+                    nc.scalar.copy(out=res[:, r0 : r0 + per_bank, :], in_=acc[:])
+                if r0 + per_bank == per_store:
+                    nc.sync.dma_start(out_view[:, g0 - r0 : g0 - r0 + per_store, tok], res[:])
 
-        permute_wk(1, wk_raw1)
         squares(0, 0, (0, 1,))
         squares(0, 0, (2, 3,))
-        cauchy(0, 0, 0, 2, "S")
-        squares(1, 0, (2, 3,))
-        squares(0, 1, (0, 1,))
-        cauchy(0, 0, 2, 4, "S")
-        squares(1, 1, (0, 1,))
-        squares(1, 0, (0, 1,))
         quant_wf(0, 0)
+        permute_wk(1, wk_raw1)
         quant_wf(1, 0)
+        cauchy(0, 0, 0, 2, "S")
         hidden(0, 0, 0, 2)
-        squares(0, 1, (2, 3,))
+        squares(1, 0, (0, 1,))
+        cauchy(0, 0, 2, 4, "S")
+        hidden(0, 0, 2, 4)
+        squares(1, 0, (2, 3,))
         quant_wf(0, 1)
         quant_wf(1, 1)
-        quant_wm(0)
-        cauchy(1, 0, 0, 2, "S")
-        cauchy(1, 0, 2, 4, "V")
-        cauchy(0, 1, 0, 2, "S")
-        hidden(0, 0, 2, 4)
-        squares(1, 1, (2, 3,))
+        squares(0, 1, (0, 1,))
+        cauchy(1, 0, 0, 2, "V")
         hidden(1, 0, 0, 2)
+        squares(0, 1, (2, 3,))
+        quant_wm(0)
         quant_wm(1)
+        squares(1, 1, (0, 1,))
+        cauchy(1, 0, 2, 4, "S")
         hidden(1, 0, 2, 4)
-        cauchy(0, 1, 2, 4, "S")
+        squares(1, 1, (2, 3,))
+        mix(0, 0, 2, "vv")
+        cauchy(0, 1, 0, 2, "V")
         hidden(0, 1, 0, 2)
-        hidden(0, 1, 2, 4)
-        mix(0, 0, 2, "vs")
         cauchy(1, 1, 0, 2, "S")
-        cauchy(1, 1, 2, 3, "S")
         hidden(1, 1, 0, 2)
-        mix(0, 2, 4, "sv")
+        mix(0, 2, 4, "ss")
+        cauchy(0, 1, 2, 4, "S")
+        hidden(0, 1, 2, 4)
         mix(1, 0, 2, "ss")
+        cauchy(1, 1, 2, 3, "S")
         hidden(1, 1, 2, 3)
-        mix(1, 2, 3, "v")
         cauchy(1, 1, 3, 4, "S")
         hidden(1, 1, 3, 4)
-        mix(1, 3, 4, "v")
+        mix(1, 2, 3, "s")
+        mix(1, 3, 4, "svsv")

@@ -31,9 +31,10 @@ def tile_list_ball_cauchy_mix_kernel(tc, tab_words, tab_scales, offs, wk_words, 
         cast = ctx.enter_context(tc.tile_pool(name="cast", bufs=3))
         hpool = ctx.enter_context(tc.tile_pool(name="hpool", bufs=3))
         opool = ctx.enter_context(tc.tile_pool(name="opool", bufs=6))
-        xps = ctx.enter_context(tc.psum_pool(name="xps", bufs=2))
-        fps = ctx.enter_context(tc.psum_pool(name="fps", bufs=3))
-        ops = ctx.enter_context(tc.psum_pool(name="ops", bufs=3))
+        psum = ctx.enter_context(tc.psum_pool(name="psum", bufs=1))
+
+        def bank(i, shape):
+            return psum.tile(shape, F32, name="bank%d" % i, tag="bank%d" % i)
 
         offsets = keep.tile([P, S // 16], U16, name="offsets")
         nc.sync.dma_start(offsets[:], offs)
@@ -48,8 +49,10 @@ def tile_list_ball_cauchy_mix_kernel(tc, tab_words, tab_scales, offs, wk_words, 
         nc.scalar.activation(out=warm[:, 1:2], in_=warm[:, 0:1], func=ACT.Abs_reciprocal_sqrt)
 
         bias = keep.tile([P, 2, 8], F32, name="bias", align_bytes=64)
-        for e in range(2):
-            nc.gpsimd.dma_start(bias[e:P:2, :, 0:7], bk.rearrange("(b u k) -> u b k", b=2, k=8)[:, :, e : e + 7])
+        with nc.allow_non_contiguous_dma(reason="one bias value for each partition and slot"):
+            for b in range(2):
+                for e in range(2):
+                    nc.gpsimd.dma_start(bias[e:P:2, b, 0:PACK], bk.rearrange("(b u t e) -> b e u t", b=2, t=PACK, e=2)[b, e])
 
         wk_view = wk_words.rearrange("a p c -> p a c")
         wkp = [keep.tile([P, 2, PASS // 2], I32, name="wkp%d" % b, align_bytes=64) for b in range(2)]
@@ -74,8 +77,9 @@ def tile_list_ball_cauchy_mix_kernel(tc, tab_words, tab_scales, offs, wk_words, 
         nc.vector.memset(tscale[64:128, :], 0)
         nc.vector.memset(kscale_raw[32:64, :], 0)
         nc.vector.memset(kscale_raw[64:128, :], 0)
-        planes = keep.tile([P, 2, (S + H) // 4], I32, name="planes", align_bytes=64)
-        nc.vector.memset(planes[:], 0)
+        planes = [keep.tile([P, (S + H) // 4], I32, name="plane%d" % a, align_bytes=64) for a in range(2)]
+        for a in range(2):
+            nc.vector.memset(planes[a][:], 0)
 
         picked = keep.tile([P, S // 4], I32, name="picked", align_bytes=64)
         nc.vector.tensor_copy(picked[:].bitcast(U8), tscale[:].bitcast(U8).indirect(offsets[:]))
@@ -87,11 +91,11 @@ def tile_list_ball_cauchy_mix_kernel(tc, tab_words, tab_scales, offs, wk_words, 
         )
         nc.vector.tensor_copy(rows[0:32, 0 : S // 4], picked[0:32, :])
         permute_wk(0, wk_raw0[:])
-        nc.vector.tensor_copy(planes[0:32, 0, :], rows[0:32, :])
+        nc.vector.tensor_copy(planes[0][0:32, :], rows[0:32, :])
         for row in range(4, 32, 4):
             a, q = divmod(row // 4, 4)
-            queue = nc.gpsimd if row == 4 else nc.scalar
-            queue.dma_start(planes[32 * q : 32 * q + 4, a, :], rows[row : row + 4, :])
+            queue = nc.gpsimd if row == 28 else nc.scalar
+            queue.dma_start(planes[a][32 * q : 32 * q + 4, :], rows[row : row + 4, :])
 
         slot = 4 * PACK * HALF
         wk_late = stage.tile([P, 2, PASS // 2], I32, name="wk_late", align_bytes=64, offset=6 * slot)
@@ -113,77 +117,90 @@ def tile_list_ball_cauchy_mix_kernel(tc, tab_words, tab_scales, offs, wk_words, 
                 nc.sync.dma_start(raw_slot(4 + b)[e:P:2], src[e])
 
         vw = [keep.tile([P, S], I32, name="vw%d" % a, align_bytes=64) for a in range(2)]
-        nc.vector.tensor_copy(vw[0][:].bitcast(U32), table[0][:].bitcast(U32).indirect(offsets[:]))
-        for h in range(2):
-            nc.vector.tensor_copy(
-                vw[1][:, h * HALF : (h + 1) * HALF].bitcast(U32),
-                table[1][:].bitcast(U32).indirect(offsets[:, h * HALF // 16 : (h + 1) * HALF // 16]),
-            )
-        planes8 = planes[:].bitcast(U8)
+        for a in range(2):
+            for h in range(2):
+                nc.vector.tensor_copy(
+                    vw[a][:, h * HALF : (h + 1) * HALF].bitcast(U32),
+                    table[a][:].bitcast(U32).indirect(offsets[:, h * HALF // 16 : (h + 1) * HALF // 16]),
+                )
+        planes8 = [planes[a][:].bitcast(U8) for a in range(2)]
 
         wfq = {}
         wmq = {}
+        grouped = {}
 
-        def quant_wf(a, b):
+        def cast_wf(a, b):
             g = cast.tile([P, PACK * PASS], BF16, name="grouped", tag="grouped", align_bytes=64)
             nc.vector.tensor_copy(
                 out=g[:].rearrange("p (t u e j) -> p t u j e", t=PACK, e=2, j=PACK),
                 in_=raw_slot(2 * b + a).rearrange("p j (u t e) -> p t u j e", t=PACK, e=2),
             )
+            grouped["f", a, b] = g
+
+        def quant_wf(a, b):
             codes = keep.tile([P, PASS], U32, name="wfc%d%d" % (a, b), align_bytes=64)
             scales = keep.tile([P, PASS], U8, name="wfs%d%d" % (a, b), align_bytes=64)
-            nc.vector.quantize_mx(out=codes[:].bitcast(FP8X4), scales=scales[:], in_=g[:])
+            nc.vector.quantize_mx(out=codes[:].bitcast(FP8X4), scales=scales[:], in_=grouped["f", a, b][:])
             wfq[a, b] = (codes, scales)
 
-        def quant_wm(b):
+        def cast_wm(b):
             g = cast.tile([P, PACK * N], BF16, name="grouped", tag="grouped", align_bytes=64)
             nc.vector.tensor_copy(
                 out=g[:].rearrange("p (c i j) -> p c j i", i=2, j=PACK),
                 in_=raw_slot(4 + b).rearrange("p j (c i) -> p c j i", i=2),
             )
+            grouped["m", b] = g
+
+        def quant_wm(b):
             codes = keep.tile([P, N], U32, name="wmc%d" % b, align_bytes=64)
             scales = keep.tile([P, N], U8, name="wms%d" % b, align_bytes=64)
-            nc.vector.quantize_mx(out=codes[:].bitcast(FP8X4), scales=scales[:], in_=g[:])
+            nc.vector.quantize_mx(out=codes[:].bitcast(FP8X4), scales=scales[:], in_=grouped["m", b][:])
             wmq[b] = (codes, scales)
 
-        ys = {
-            (b, h): keep.tile([P, HALF // CHUNK, PACK, CHUNK], F32, name="y%d%d" % (b, h))
-            for b in range(2)
-            for h in range(2)
-        }
+        ys = [keep.tile([P, HALF // CHUNK, PACK, CHUNK], F32, name="y%d" % q) for q in range(4)]
+        xs = {}
+        fs = {}
+        hbs = {}
 
-        def squares(b, h, slots):
-            y = ys[b, h]
+        def project(q, t, passes):
+            b, h = divmod(q, 2)
             tok = slice(h * HALF, (h + 1) * HALF)
-            for t in slots:
-                if (b, h) == (0, 0) and t >= 2:
-                    x = ops.tile([P, HALF], F32, name="acc", tag="acc")
-                else:
-                    x = xps.tile([P, HALF], F32, name="x", tag="x")
-                for a in range(2):
-                    c0 = S + b * PASS + t * P
-                    nc.tensor.matmul_mx(
-                        out=x[:],
-                        lhsT=wkp[b][:, a, t * P // 2 : (t + 1) * P // 2].bitcast(U8).bitcast(FP4X4),
-                        lhsT_scale=planes8[:, a, c0 : c0 + P],
-                        rhs=vw[a][:, tok].bitcast(FP8X4),
-                        rhs_scale=planes8[:, a, tok],
-                        start=(a == 0),
-                        stop=(a == 1),
-                    )
-                nc.scalar.activation(
-                    out=y[:, :, t, :],
-                    in_=x[:].rearrange("p (c n) -> p c n", n=CHUNK),
-                    func=ACT.Square,
-                    bias=bias[:, b, 2 * t : 2 * t + 1],
+            if (q, t) not in xs:
+                xs[q, t] = bank(t, [P, HALF])
+            for a in passes:
+                c0 = S + b * PASS + t * P
+                nc.tensor.matmul_mx(
+                    out=xs[q, t][:],
+                    lhsT=wkp[b][:, a, t * P // 2 : (t + 1) * P // 2].bitcast(U8).bitcast(FP4X4),
+                    lhsT_scale=planes8[a][:, c0 : c0 + P],
+                    rhs=vw[a][:, tok].bitcast(FP8X4),
+                    rhs_scale=planes8[a][:, tok],
+                    start=(a == 0),
+                    stop=(a == 1),
                 )
 
-        def cauchy(b, h, c0, c1, eng):
-            part = ys[b, h][:, c0:c1, :, :].rearrange("p c t n -> p (c t n)")
+        def square(q, t):
+            nc.scalar.activation(
+                out=ys[q][:, :, t, :],
+                in_=xs[q, t][:].rearrange("p (c n) -> p c n", n=CHUNK),
+                func=ACT.Square,
+                bias=bias[:, q // 2, t : t + 1],
+            )
+            if q <= 2:
+                project(q + 1, t, (0, 1))
+
+        def gate(q, c0, c1):
+            return ys[q][:, c0:c1, :, :].rearrange("p c t n -> p (c t n)")
+
+        def root(q, c0, c1):
+            part = gate(q, c0, c1)
             nc.scalar.activation(out=part, in_=part, func=ACT.Abs_reciprocal_sqrt, bias=1.0)
-            if eng == "S":
+
+        def unroot(q, c0, c1, eng):
+            part = gate(q, c0, c1)
+            if eng == "s":
                 nc.scalar.activation(out=part, in_=part, func=ACT.Square)
-            elif eng == "V":
+            elif eng == "v":
                 nc.vector.tensor_tensor(out=part, in0=part, in1=part, op=MULT)
             else:
                 nc.gpsimd.tensor_tensor(out=part, in0=part, in1=part, op=MULT)
@@ -191,103 +208,141 @@ def tile_list_ball_cauchy_mix_kernel(tc, tab_words, tab_scales, offs, wk_words, 
         hc = [keep.tile([P, S], U32, name="hc%d" % b, align_bytes=64) for b in range(2)]
         hs = [keep.tile([P, S], U8, name="hs%d" % b, align_bytes=64) for b in range(2)]
 
-        def hidden(b, h, c0, c1):
-            hb = hpool.tile([P, c1 - c0, CHUNK * PACK], BF16, name="hb", tag="hb", align_bytes=64)
-            for c in range(c0, c1):
-                tok = slice(h * HALF + c * CHUNK, h * HALF + (c + 1) * CHUNK)
-                f = fps.tile([P, PACK, CHUNK], F32, name="f")
-                for t in range(PACK):
-                    for a in range(2):
-                        codes, scales = wfq[a, b]
-                        nc.tensor.matmul_mx(
-                            out=f[:, t, :],
-                            lhsT=codes[:, t * P : (t + 1) * P].bitcast(FP8X4),
-                            lhsT_scale=scales[:, t * P : (t + 1) * P],
-                            rhs=vw[a][:, tok].bitcast(FP8X4),
-                            rhs_scale=planes8[:, a, tok],
-                            start=(a == 0),
-                            stop=(a == 1),
-                        )
-                nc.vector.tensor_tensor(
-                    out=hb[:, c - c0, :].rearrange("p (u i t) -> p u t i", i=2, t=PACK),
-                    in0=f[:].rearrange("p t (u i) -> p u t i", i=2),
-                    in1=ys[b, h][:, c, :, :].rearrange("p t (u i) -> p u t i", i=2),
-                    op=MULT,
-                )
+        def feature(q, c):
+            b, h = divmod(q, 2)
+            tok = slice(h * HALF + c * CHUNK, h * HALF + (c + 1) * CHUNK)
+            f = bank(PACK + c, [P, PACK, CHUNK])
+            for t in range(PACK):
+                for a in range(2):
+                    codes, scales = wfq[a, b]
+                    nc.tensor.matmul_mx(
+                        out=f[:, t, :],
+                        lhsT=codes[:, t * P : (t + 1) * P].bitcast(FP8X4),
+                        lhsT_scale=scales[:, t * P : (t + 1) * P],
+                        rhs=vw[a][:, tok].bitcast(FP8X4),
+                        rhs_scale=planes8[a][:, tok],
+                        start=(a == 0),
+                        stop=(a == 1),
+                    )
+            fs[q, c] = f
+
+        def weigh(q, c):
+            if c % 2 == 0:
+                hbs[q, c // 2] = hpool.tile([P, 2, CHUNK * PACK], BF16, name="hb", tag="hb", align_bytes=64)
+            nc.vector.tensor_tensor(
+                out=hbs[q, c // 2][:, c % 2, :].rearrange("p (u i t) -> p u t i", i=2, t=PACK),
+                in0=fs[q, c][:].rearrange("p t (u i) -> p u t i", i=2),
+                in1=ys[q][:, c, :, :].rearrange("p t (u i) -> p u t i", i=2),
+                op=MULT,
+            )
+            if q in (0, 2):
+                feature(q + 1, c)
+
+        def quant_h(q, c0, c1):
+            b, h = divmod(q, 2)
             tok = slice(h * HALF + c0 * CHUNK, h * HALF + c1 * CHUNK)
+            src = hbs[q, c0 // 2][:, c0 % 2 : c0 % 2 + c1 - c0, :]
             nc.vector.quantize_mx(
-                out=hc[b][:, tok].bitcast(FP8X4), scales=hs[b][:, tok], in_=hb[:].rearrange("p c w -> p (c w)")
+                out=hc[b][:, tok].bitcast(FP8X4), scales=hs[b][:, tok], in_=src.rearrange("p c w -> p (c w)")
             )
 
         out_view = out.rearrange("(g p) s -> p g s", p=P)
 
-        def mix(h, c0, c1, engines):
+        def mix(h, c0, c1, g0, g1, i):
             width = (c1 - c0) * CHUNK
             tok = slice(h * HALF + c0 * CHUNK, h * HALF + c1 * CHUNK)
-            per_bank = (N // P) // len(engines)
-            per_store = max(per_bank, 2)
-            for g0 in range(0, N // P, per_bank):
-                if g0 % per_store == 0:
-                    res = opool.tile([P, per_store, width], F32, name="res", tag="res")
-                if per_bank == 1 and g0 % 2 == 1:
-                    acc = xps.tile([P, per_bank, width], F32, name="x", tag="x")
-                else:
-                    acc = ops.tile([P, per_bank, width], F32, name="acc", tag="acc")
-                for g in range(g0, g0 + per_bank):
-                    for b in range(2):
-                        codes, scales = wmq[b]
-                        nc.tensor.matmul_mx(
-                            out=acc[:, g - g0, :],
-                            lhsT=codes[:, g * P : (g + 1) * P].bitcast(FP8X4),
-                            lhsT_scale=scales[:, g * P : (g + 1) * P],
-                            rhs=hc[b][:, tok].bitcast(FP8X4),
-                            rhs_scale=hs[b][:, tok],
-                            start=(b == 0),
-                            stop=(b == 1),
-                        )
-                r0 = g0 % per_store
-                if engines[g0 // per_bank] == "v":
-                    nc.vector.tensor_copy(out=res[:, r0 : r0 + per_bank, :], in_=acc[:])
-                else:
-                    nc.scalar.copy(out=res[:, r0 : r0 + per_bank, :], in_=acc[:])
-                if r0 + per_bank == per_store:
-                    nc.sync.dma_start(out_view[:, g0 - r0 : g0 - r0 + per_store, tok], res[:])
+            acc = bank(i, [P, g1 - g0, width])
+            for g in range(g0, g1):
+                for b in range(2):
+                    codes, scales = wmq[b]
+                    nc.tensor.matmul_mx(
+                        out=acc[:, g - g0, :],
+                        lhsT=codes[:, g * P : (g + 1) * P].bitcast(FP8X4),
+                        lhsT_scale=scales[:, g * P : (g + 1) * P],
+                        rhs=hc[b][:, tok].bitcast(FP8X4),
+                        rhs_scale=hs[b][:, tok],
+                        start=(b == 0),
+                        stop=(b == 1),
+                    )
+            return acc, out_view[:, g0:g1, tok]
 
-        squares(0, 0, (0, 1,))
-        squares(0, 0, (2, 3,))
-        quant_wf(0, 0)
+        def store(mixed, eng):
+            acc, dst = mixed
+            res = opool.tile(list(acc.shape), F32, name="res", tag="res")
+            if eng == "v":
+                nc.vector.tensor_copy(out=res[:], in_=acc[:])
+            else:
+                nc.scalar.copy(out=res[:], in_=acc[:])
+            nc.sync.dma_start(dst, res[:])
+
+        for t in range(PACK):
+            project(0, t, (0,))
+        for t in range(PACK):
+            project(0, t, (1,))
+            square(0, t)
+        cast_wf(0, 0)
         permute_wk(1, wk_raw1)
+        quant_wf(0, 0)
+        square(1, 0)
+        root(0, 0, 2)
+        root(0, 2, 4)
+        cast_wf(1, 0)
+        unroot(0, 0, 2, "v")
         quant_wf(1, 0)
-        cauchy(0, 0, 0, 2, "S")
-        hidden(0, 0, 0, 2)
-        squares(1, 0, (0, 1,))
-        cauchy(0, 0, 2, 4, "S")
-        hidden(0, 0, 2, 4)
-        squares(1, 0, (2, 3,))
-        quant_wf(0, 1)
-        quant_wf(1, 1)
-        squares(0, 1, (0, 1,))
-        cauchy(1, 0, 0, 2, "V")
-        hidden(1, 0, 0, 2)
-        squares(0, 1, (2, 3,))
+        for c in range(4):
+            feature(0, c)
+        unroot(0, 2, 4, "v")
+        for t in range(1, PACK):
+            square(1, t)
+
+        for q in range(2):
+            square(q + 2, 0)
+            root(q + 1, 0, 2)
+            root(q + 1, 2, 4)
+            weigh(q, 0)
+            weigh(q, 1)
+            cast_wf(q, 1)
+            quant_h(q, 0, 2)
+            unroot(q + 1, 0, 2, "s")
+            weigh(q, 2)
+            weigh(q, 3)
+            quant_wf(q, 1)
+            quant_h(q, 2, 4)
+            for t in range(1, PACK):
+                square(q + 2, t)
+            unroot(q + 1, 2, 4, "s")
+        for c in range(4):
+            feature(2, c)
+        cast_wm(0)
+        root(3, 0, 2)
+        root(3, 2, 4)
+        weigh(2, 0)
+        weigh(2, 1)
         quant_wm(0)
+        quant_h(2, 0, 2)
+        cast_wm(1)
+        unroot(3, 0, 2, "s")
+        weigh(2, 2)
+        weigh(2, 3)
         quant_wm(1)
-        squares(1, 1, (0, 1,))
-        cauchy(1, 0, 2, 4, "S")
-        hidden(1, 0, 2, 4)
-        squares(1, 1, (2, 3,))
-        mix(0, 0, 2, "vv")
-        cauchy(0, 1, 0, 2, "V")
-        hidden(0, 1, 0, 2)
-        cauchy(1, 1, 0, 2, "S")
-        hidden(1, 1, 0, 2)
-        mix(0, 2, 4, "ss")
-        cauchy(0, 1, 2, 4, "S")
-        hidden(0, 1, 2, 4)
-        mix(1, 0, 2, "ss")
-        cauchy(1, 1, 2, 3, "S")
-        hidden(1, 1, 2, 3)
-        cauchy(1, 1, 3, 4, "S")
-        hidden(1, 1, 3, 4)
-        mix(1, 2, 3, "s")
-        mix(1, 3, 4, "svsv")
+        quant_h(2, 2, 4)
+        unroot(3, 2, 3, "s")
+        unroot(3, 3, 4, "s")
+        first = [mix(0, 0, 4, g, g + 1, g) for g in range(4)]
+        weigh(3, 0)
+        weigh(3, 1)
+        weigh(3, 2)
+        quant_h(3, 0, 2)
+        second = [mix(1, 0, 2, 2 * j, 2 * j + 2, PACK + j) for j in range(2)]
+        weigh(3, 3)
+        quant_h(3, 2, 3)
+        third = mix(1, 2, 3, 0, 4, 6)
+        quant_h(3, 3, 4)
+        for g in range(4):
+            store(first[g], "s")
+        last = [mix(1, 3, 4, 2 * j, 2 * j + 2, (7 + j) % 8) for j in range(2)]
+        store(second[0], "v")
+        store(second[1], "s")
+        store(third, "v")
+        store(last[0], "s")
+        store(last[1], "v")

@@ -49,10 +49,8 @@ def tile_list_ball_cauchy_mix_kernel(tc, tab_words, tab_scales, offs, wk_words, 
         nc.scalar.activation(out=warm[:, 1:2], in_=warm[:, 0:1], func=ACT.Abs_reciprocal_sqrt)
 
         bias = keep.tile([P, 2, 8], F32, name="bias", align_bytes=64)
-        with nc.allow_non_contiguous_dma(reason="one bias value for each partition and slot"):
-            for b in range(2):
-                for e in range(2):
-                    nc.gpsimd.dma_start(bias[e:P:2, b, 0:PACK], bk.rearrange("(b u t e) -> b e u t", b=2, t=PACK, e=2)[b, e])
+        for e in range(2):
+            nc.gpsimd.dma_start(bias[e:P:2, :, 0:7], bk.rearrange("(b u k) -> u b k", b=2, k=8)[:, :, e : e + 7])
 
         wk_view = wk_words.rearrange("a p c -> p a c")
         wkp = [keep.tile([P, 2, PASS // 2], I32, name="wkp%d" % b, align_bytes=64) for b in range(2)]
@@ -69,7 +67,9 @@ def tile_list_ball_cauchy_mix_kernel(tc, tab_words, tab_scales, offs, wk_words, 
             )
 
         wk_raw0 = load_wk(0)
-        table = [keep.tile([P, T], I32, name="table%d" % a, align_bytes=64) for a in range(2)]
+        slot = 4 * PACK * HALF
+        wk_bytes = 4 * PASS
+        table = [stage.tile([P, T], I32, name="table%d" % a, align_bytes=64, offset=a * (2 * slot + wk_bytes)) for a in range(2)]
         for a in range(2):
             nc.sync.dma_start(table[a][:], tab_words[a].rearrange("p n t -> p (n t)").bitcast(I32))
 
@@ -83,8 +83,7 @@ def tile_list_ball_cauchy_mix_kernel(tc, tab_words, tab_scales, offs, wk_words, 
 
         picked = keep.tile([P, S // 4], I32, name="picked", align_bytes=64)
         nc.vector.tensor_copy(picked[:].bitcast(U8), tscale[:].bitcast(U8).indirect(offsets[:]))
-        region = stage.tile([P, 6 * PACK * HALF + PASS], I32, name="region", align_bytes=64, offset=0)
-        rows = region[:, 0 : (S + H) // 4]
+        rows = keep.tile([P, (S + H) // 4], I32, name="rows", align_bytes=64)
         nc.vector.tensor_copy(
             out=rows[:, S // 4 :].bitcast(U16).rearrange("p (b t u) -> p b t u", b=2, t=PACK),
             in_=kscale_raw[:].bitcast(U16).rearrange("p (b u t) -> p b t u", b=2, t=PACK),
@@ -97,10 +96,19 @@ def tile_list_ball_cauchy_mix_kernel(tc, tab_words, tab_scales, offs, wk_words, 
             queue = nc.gpsimd if row == 28 else nc.scalar
             queue.dma_start(planes[a][32 * q : 32 * q + 4, :], rows[row : row + 4, :])
 
-        slot = 4 * PACK * HALF
-        wk_late = stage.tile([P, 2, PASS // 2], I32, name="wk_late", align_bytes=64, offset=6 * slot)
+        vw = [keep.tile([P, S], I32, name="vw%d" % a, align_bytes=64) for a in range(2)]
+        for a in range(2):
+            for h in range(2):
+                nc.vector.tensor_copy(
+                    vw[a][:, h * HALF : (h + 1) * HALF].bitcast(U32),
+                    table[a][:].bitcast(U32).indirect(offsets[:, h * HALF // 16 : (h + 1) * HALF // 16]),
+                )
+        planes8 = [planes[a][:].bitcast(U8) for a in range(2)]
+
+        wk_late = stage.tile([P, 2, PASS // 2], I32, name="wk_late", align_bytes=64, offset=slot)
         wk_raw1 = wk_late[:]
-        raws = [stage.tile([P, PACK, HALF], F32, name="raw%d" % i, align_bytes=64, offset=i * slot) for i in range(6)]
+        places = [0, slot + wk_bytes, 2 * slot + wk_bytes, 3 * slot + wk_bytes, 0, slot + wk_bytes]
+        raws = [stage.tile([P, PACK, HALF], F32, name="raw%d" % i, align_bytes=64, offset=places[i]) for i in range(6)]
 
         def raw_slot(i):
             return raws[i][:]
@@ -111,19 +119,11 @@ def tile_list_ball_cauchy_mix_kernel(tc, tab_words, tab_scales, offs, wk_words, 
                 nc.sync.dma_start(raw_slot(2 * b + a), src.rearrange("(p j) c -> p j c", j=PACK))
                 if (a, b) == (0, 0):
                     nc.sync.dma_start(wk_raw1, wk_view[:, :, 2 * PASS : 4 * PASS].bitcast(I32))
-        for b in range(2):
+
+        def load_wm(b):
             src = wm[b * PASS : (b + 1) * PASS, :].rearrange("(u t e) c -> e u t c", t=PACK, e=2)
             for e in range(2):
                 nc.sync.dma_start(raw_slot(4 + b)[e:P:2], src[e])
-
-        vw = [keep.tile([P, S], I32, name="vw%d" % a, align_bytes=64) for a in range(2)]
-        for a in range(2):
-            for h in range(2):
-                nc.vector.tensor_copy(
-                    vw[a][:, h * HALF : (h + 1) * HALF].bitcast(U32),
-                    table[a][:].bitcast(U32).indirect(offsets[:, h * HALF // 16 : (h + 1) * HALF // 16]),
-                )
-        planes8 = [planes[a][:].bitcast(U8) for a in range(2)]
 
         wfq = {}
         wmq = {}
@@ -136,6 +136,8 @@ def tile_list_ball_cauchy_mix_kernel(tc, tab_words, tab_scales, offs, wk_words, 
                 in_=raw_slot(2 * b + a).rearrange("p j (u t e) -> p t u j e", t=PACK, e=2),
             )
             grouped["f", a, b] = g
+            if b == 0:
+                load_wm(a)
 
         def quant_wf(a, b):
             codes = keep.tile([P, PASS], U32, name="wfc%d%d" % (a, b), align_bytes=64)
@@ -184,26 +186,28 @@ def tile_list_ball_cauchy_mix_kernel(tc, tab_words, tab_scales, offs, wk_words, 
                 out=ys[q][:, :, t, :],
                 in_=xs[q, t][:].rearrange("p (c n) -> p c n", n=CHUNK),
                 func=ACT.Square,
-                bias=bias[:, q // 2, t : t + 1],
+                bias=bias[:, q // 2, 2 * t : 2 * t + 1],
             )
             if q <= 2:
                 project(q + 1, t, (0, 1))
+
+        roots = [keep.tile([P, HALF * PACK], F32, name="root%d" % q) for q in range(4)]
 
         def gate(q, c0, c1):
             return ys[q][:, c0:c1, :, :].rearrange("p c t n -> p (c t n)")
 
         def root(q, c0, c1):
-            part = gate(q, c0, c1)
-            nc.scalar.activation(out=part, in_=part, func=ACT.Abs_reciprocal_sqrt, bias=1.0)
+            part = roots[q][:, c0 * PASS : c1 * PASS]
+            nc.scalar.activation(out=part, in_=gate(q, c0, c1), func=ACT.Abs_reciprocal_sqrt, bias=1.0)
 
         def unroot(q, c0, c1, eng):
-            part = gate(q, c0, c1)
+            part = roots[q][:, c0 * PASS : c1 * PASS]
             if eng == "s":
-                nc.scalar.activation(out=part, in_=part, func=ACT.Square)
+                nc.scalar.activation(out=gate(q, c0, c1), in_=part, func=ACT.Square)
             elif eng == "v":
-                nc.vector.tensor_tensor(out=part, in0=part, in1=part, op=MULT)
+                nc.vector.tensor_tensor(out=gate(q, c0, c1), in0=part, in1=part, op=MULT)
             else:
-                nc.gpsimd.tensor_tensor(out=part, in0=part, in1=part, op=MULT)
+                nc.gpsimd.tensor_tensor(out=gate(q, c0, c1), in0=part, in1=part, op=MULT)
 
         hc = [keep.tile([P, S], U32, name="hc%d" % b, align_bytes=64) for b in range(2)]
         hs = [keep.tile([P, S], U8, name="hs%d" % b, align_bytes=64) for b in range(2)]
@@ -265,6 +269,21 @@ def tile_list_ball_cauchy_mix_kernel(tc, tab_words, tab_scales, offs, wk_words, 
                         stop=(b == 1),
                     )
             return acc, out_view[:, g0:g1, tok]
+
+        def mix_pass(acc, h, c, g0, b):
+            tok = slice(h * HALF + c * CHUNK, h * HALF + (c + 1) * CHUNK)
+            codes, scales = wmq[b]
+            for g in range(g0, g0 + 2):
+                nc.tensor.matmul_mx(
+                    out=acc[:, g - g0, :],
+                    lhsT=codes[:, g * P : (g + 1) * P].bitcast(FP8X4),
+                    lhsT_scale=scales[:, g * P : (g + 1) * P],
+                    rhs=hc[b][:, tok].bitcast(FP8X4),
+                    rhs_scale=hs[b][:, tok],
+                    start=(b == 0 and g == g0),
+                    stop=(b == 1 and g == g0 + 1),
+                )
+            return acc, out_view[:, g0 : g0 + 2, tok]
 
         def store(mixed, eng):
             acc, dst = mixed
@@ -337,10 +356,13 @@ def tile_list_ball_cauchy_mix_kernel(tc, tab_words, tab_scales, offs, wk_words, 
         weigh(3, 3)
         quant_h(3, 2, 3)
         third = mix(1, 2, 3, 0, 4, 6)
-        quant_h(3, 3, 4)
         for g in range(4):
             store(first[g], "s")
-        last = [mix(1, 3, 4, 2 * j, 2 * j + 2, (7 + j) % 8) for j in range(2)]
+        accs = [bank(j, [P, 2, CHUNK]) for j in range(2)]
+        for j in range(2):
+            mix_pass(accs[j], 1, 3, 2 * j, 0)
+        quant_h(3, 3, 4)
+        last = [mix_pass(accs[j], 1, 3, 2 * j, 1) for j in range(2)]
         store(second[0], "v")
         store(second[1], "s")
         store(third, "v")

@@ -97,11 +97,12 @@ def tile_list_ball_cauchy_mix_kernel(tc, tab_words, tab_scales, offs, wk_words, 
             queue.dma_start(planes[a][32 * q : 32 * q + 4, :], rows[row : row + 4, :])
 
         vw = [keep.tile([P, S], I32, name="vw%d" % a, align_bytes=64) for a in range(2)]
+        cuts = [(0, HALF, S), (0, HALF // 2, HALF, S)]
         for a in range(2):
-            for h in range(2):
+            for j0, j1 in zip(cuts[a], cuts[a][1:]):
                 nc.vector.tensor_copy(
-                    vw[a][:, h * HALF : (h + 1) * HALF].bitcast(U32),
-                    table[a][:].bitcast(U32).indirect(offsets[:, h * HALF // 16 : (h + 1) * HALF // 16]),
+                    vw[a][:, j0:j1].bitcast(U32),
+                    table[a][:].bitcast(U32).indirect(offsets[:, j0 // 16 : j1 // 16]),
                 )
         planes8 = [planes[a][:].bitcast(U8) for a in range(2)]
 
@@ -117,7 +118,7 @@ def tile_list_ball_cauchy_mix_kernel(tc, tab_words, tab_scales, offs, wk_words, 
             for a in range(2):
                 src = wf[a * PASS : (a + 1) * PASS, b * PASS : (b + 1) * PASS]
                 nc.sync.dma_start(raw_slot(2 * b + a), src.rearrange("(p j) c -> p j c", j=PACK))
-                if (a, b) == (0, 0):
+                if (a, b) == (1, 0):
                     nc.sync.dma_start(wk_raw1, wk_view[:, :, 2 * PASS : 4 * PASS].bitcast(I32))
 
         def load_wm(b):
@@ -164,31 +165,31 @@ def tile_list_ball_cauchy_mix_kernel(tc, tab_words, tab_scales, offs, wk_words, 
         fs = {}
         hbs = {}
 
-        def project(q, t, passes):
+        def project(q, t, passes, c0=0, c1=4, first_bank=0, first=0):
             b, h = divmod(q, 2)
-            tok = slice(h * HALF, (h + 1) * HALF)
-            if (q, t) not in xs:
-                xs[q, t] = bank(t, [P, HALF])
+            tok = slice(h * HALF + c0 * CHUNK, h * HALF + c1 * CHUNK)
+            if (q, t, c0) not in xs:
+                xs[q, t, c0] = bank(first_bank + t, [P, (c1 - c0) * CHUNK])
             for a in passes:
-                c0 = S + b * PASS + t * P
+                k0 = S + b * PASS + t * P
                 nc.tensor.matmul_mx(
-                    out=xs[q, t][:],
+                    out=xs[q, t, c0][:],
                     lhsT=wkp[b][:, a, t * P // 2 : (t + 1) * P // 2].bitcast(U8).bitcast(FP4X4),
-                    lhsT_scale=planes8[a][:, c0 : c0 + P],
+                    lhsT_scale=planes8[a][:, k0 : k0 + P],
                     rhs=vw[a][:, tok].bitcast(FP8X4),
                     rhs_scale=planes8[a][:, tok],
-                    start=(a == 0),
-                    stop=(a == 1),
+                    start=(a == first),
+                    stop=(a != first),
                 )
 
-        def square(q, t):
+        def square(q, t, c0=0, c1=4):
             nc.scalar.activation(
-                out=ys[q][:, :, t, :],
-                in_=xs[q, t][:].rearrange("p (c n) -> p c n", n=CHUNK),
+                out=ys[q][:, c0:c1, t, :],
+                in_=xs[q, t, c0][:].rearrange("p (c n) -> p c n", n=CHUNK),
                 func=ACT.Square,
                 bias=bias[:, q // 2, 2 * t : 2 * t + 1],
             )
-            if q <= 2:
+            if q <= 2 and c1 == 4:
                 project(q + 1, t, (0, 1))
 
         roots = [keep.tile([P, HALF * PACK], F32, name="root%d" % q) for q in range(4)]
@@ -212,23 +213,23 @@ def tile_list_ball_cauchy_mix_kernel(tc, tab_words, tab_scales, offs, wk_words, 
         hc = [keep.tile([P, S], U32, name="hc%d" % b, align_bytes=64) for b in range(2)]
         hs = [keep.tile([P, S], U8, name="hs%d" % b, align_bytes=64) for b in range(2)]
 
-        def feature(q, c):
+        def feature(q, c, passes=(0, 1)):
             b, h = divmod(q, 2)
             tok = slice(h * HALF + c * CHUNK, h * HALF + (c + 1) * CHUNK)
-            f = bank(PACK + c, [P, PACK, CHUNK])
-            for t in range(PACK):
-                for a in range(2):
-                    codes, scales = wfq[a, b]
+            if (q, c) not in fs:
+                fs[q, c] = bank(PACK + c, [P, PACK, CHUNK])
+            for a in passes:
+                codes, scales = wfq[a, b]
+                for t in range(PACK):
                     nc.tensor.matmul_mx(
-                        out=f[:, t, :],
+                        out=fs[q, c][:, t, :],
                         lhsT=codes[:, t * P : (t + 1) * P].bitcast(FP8X4),
                         lhsT_scale=scales[:, t * P : (t + 1) * P],
                         rhs=vw[a][:, tok].bitcast(FP8X4),
                         rhs_scale=planes8[a][:, tok],
-                        start=(a == 0),
-                        stop=(a == 1),
+                        start=(a == 0 and t == 0),
+                        stop=(a == 1 and t == PACK - 1),
                     )
-            fs[q, c] = f
 
         def weigh(q, c):
             if c % 2 == 0:
@@ -239,7 +240,7 @@ def tile_list_ball_cauchy_mix_kernel(tc, tab_words, tab_scales, offs, wk_words, 
                 in1=ys[q][:, c, :, :].rearrange("p t (u i) -> p u t i", i=2),
                 op=MULT,
             )
-            if q in (0, 2):
+            if q <= 2:
                 feature(q + 1, c)
 
         def quant_h(q, c0, c1):
@@ -252,28 +253,14 @@ def tile_list_ball_cauchy_mix_kernel(tc, tab_words, tab_scales, offs, wk_words, 
 
         out_view = out.rearrange("(g p) s -> p g s", p=P)
 
-        def mix(h, c0, c1, g0, g1, i):
-            width = (c1 - c0) * CHUNK
+        def piece(h, c0, c1, g0, g1, i):
             tok = slice(h * HALF + c0 * CHUNK, h * HALF + c1 * CHUNK)
-            acc = bank(i, [P, g1 - g0, width])
-            for g in range(g0, g1):
-                for b in range(2):
-                    codes, scales = wmq[b]
-                    nc.tensor.matmul_mx(
-                        out=acc[:, g - g0, :],
-                        lhsT=codes[:, g * P : (g + 1) * P].bitcast(FP8X4),
-                        lhsT_scale=scales[:, g * P : (g + 1) * P],
-                        rhs=hc[b][:, tok].bitcast(FP8X4),
-                        rhs_scale=hs[b][:, tok],
-                        start=(b == 0),
-                        stop=(b == 1),
-                    )
-            return acc, out_view[:, g0:g1, tok]
+            return bank(i, [P, g1 - g0, (c1 - c0) * CHUNK]), tok, g0, g1
 
-        def mix_pass(acc, h, c, g0, b):
-            tok = slice(h * HALF + c * CHUNK, h * HALF + (c + 1) * CHUNK)
+        def mix(part, b):
+            acc, tok, g0, g1 = part
             codes, scales = wmq[b]
-            for g in range(g0, g0 + 2):
+            for g in range(g0, g1):
                 nc.tensor.matmul_mx(
                     out=acc[:, g - g0, :],
                     lhsT=codes[:, g * P : (g + 1) * P].bitcast(FP8X4),
@@ -281,12 +268,12 @@ def tile_list_ball_cauchy_mix_kernel(tc, tab_words, tab_scales, offs, wk_words, 
                     rhs=hc[b][:, tok].bitcast(FP8X4),
                     rhs_scale=hs[b][:, tok],
                     start=(b == 0 and g == g0),
-                    stop=(b == 1 and g == g0 + 1),
+                    stop=(b == 1 and g == g1 - 1),
                 )
-            return acc, out_view[:, g0 : g0 + 2, tok]
 
         def store(mixed, eng):
-            acc, dst = mixed
+            acc, tok, g0, g1 = mixed
+            dst = out_view[:, g0:g1, tok]
             res = opool.tile(list(acc.shape), F32, name="res", tag="res")
             if eng == "v":
                 nc.vector.tensor_copy(out=res[:], in_=acc[:])
@@ -295,76 +282,102 @@ def tile_list_ball_cauchy_mix_kernel(tc, tab_words, tab_scales, offs, wk_words, 
             nc.sync.dma_start(dst, res[:])
 
         for t in range(PACK):
-            project(0, t, (0,))
+            project(0, t, (0,), 0, 2, PACK)
         for t in range(PACK):
-            project(0, t, (1,))
-            square(0, t)
+            project(0, t, (1,), 0, 2, PACK)
+            square(0, t, 0, 2)
+        for t in range(PACK):
+            project(0, t, (1, 0), 2, 4, 0, 1)
         cast_wf(0, 0)
         permute_wk(1, wk_raw1)
-        quant_wf(0, 0)
-        square(1, 0)
+        square(0, 0, 2, 4)
         root(0, 0, 2)
+        unroot(0, 0, 2, "v")
+        quant_wf(0, 0)
+        for c in range(4):
+            feature(0, c, (0,))
+        for t in range(1, PACK):
+            square(0, t, 2, 4)
+        square(1, 0)
         root(0, 2, 4)
         cast_wf(1, 0)
-        unroot(0, 0, 2, "v")
+        unroot(0, 2, 4, "v")
         quant_wf(1, 0)
         for c in range(4):
-            feature(0, c)
-        unroot(0, 2, 4, "v")
+            feature(0, c, (1,))
         for t in range(1, PACK):
             square(1, t)
-
-        for q in range(2):
-            square(q + 2, 0)
-            root(q + 1, 0, 2)
-            root(q + 1, 2, 4)
-            weigh(q, 0)
-            weigh(q, 1)
-            cast_wf(q, 1)
-            quant_h(q, 0, 2)
-            unroot(q + 1, 0, 2, "s")
-            weigh(q, 2)
-            weigh(q, 3)
-            quant_wf(q, 1)
-            quant_h(q, 2, 4)
-            for t in range(1, PACK):
-                square(q + 2, t)
-            unroot(q + 1, 2, 4, "s")
-        for c in range(4):
-            feature(2, c)
+        square(2, 0)
+        root(1, 0, 2)
+        root(1, 2, 4)
+        weigh(0, 0)
+        weigh(0, 1)
+        weigh(0, 2)
+        quant_h(0, 0, 2)
+        weigh(0, 3)
+        cast_wf(0, 1)
+        quant_h(0, 2, 4)
+        quant_wf(0, 1)
+        cast_wf(1, 1)
+        for t in range(1, PACK):
+            square(2, t)
+        unroot(1, 0, 2, "s")
+        unroot(1, 2, 4, "s")
+        quant_wf(1, 1)
+        weigh(1, 0)
+        weigh(1, 1)
+        weigh(1, 2)
+        quant_h(1, 0, 2)
+        weigh(1, 3)
+        root(2, 0, 2)
+        root(2, 2, 4)
+        for t in range(PACK):
+            square(3, t)
         cast_wm(0)
+        quant_h(1, 2, 4)
+        quant_wm(0)
+        cast_wm(1)
+        unroot(2, 0, 2, "s")
+        unroot(2, 2, 4, "s")
+        first = [piece(0, 2 * (i // 2), 2 * (i // 2) + 2, 2 * (i % 2), 2 * (i % 2) + 2, i) for i in range(4)]
+        for part in first:
+            mix(part, 0)
+        weigh(2, 0)
+        quant_wm(1)
+        weigh(2, 1)
+        weigh(2, 2)
+        quant_h(2, 0, 2)
+        mix(first[0], 1)
+        mix(first[1], 1)
+        weigh(2, 3)
         root(3, 0, 2)
         root(3, 2, 4)
-        weigh(2, 0)
-        weigh(2, 1)
-        quant_wm(0)
-        quant_h(2, 0, 2)
-        cast_wm(1)
-        unroot(3, 0, 2, "s")
-        weigh(2, 2)
-        weigh(2, 3)
-        quant_wm(1)
+        store(first[0], "v")
         quant_h(2, 2, 4)
+        mix(first[2], 1)
+        mix(first[3], 1)
+        store(first[1], "v")
+        unroot(3, 0, 2, "s")
         unroot(3, 2, 3, "s")
         unroot(3, 3, 4, "s")
-        first = [mix(0, 0, 4, g, g + 1, g) for g in range(4)]
+        last = [piece(1, 3, 4, 2 * j, 2 * j + 2, j) for j in range(2)]
+        for part in last:
+            mix(part, 0)
+        store(first[2], "s")
+        store(first[3], "s")
         weigh(3, 0)
-        weigh(3, 1)
-        weigh(3, 2)
-        quant_h(3, 0, 2)
-        second = [mix(1, 0, 2, 2 * j, 2 * j + 2, PACK + j) for j in range(2)]
-        weigh(3, 3)
-        quant_h(3, 2, 3)
-        third = mix(1, 2, 3, 0, 4, 6)
-        for g in range(4):
-            store(first[g], "s")
-        accs = [bank(j, [P, 2, CHUNK]) for j in range(2)]
-        for j in range(2):
-            mix_pass(accs[j], 1, 3, 2 * j, 0)
+        late = []
+        for c in range(3):
+            late.append(piece(1, c, c + 1, 0, 4, PACK + c))
+            mix(late[c], 0)
+            weigh(3, c + 1)
+            quant_h(3, c, c + 1)
+            mix(late[c], 1)
+        store(late[0], "s")
+        store(late[1], "s")
         quant_h(3, 3, 4)
-        last = [mix_pass(accs[j], 1, 3, 2 * j, 1) for j in range(2)]
-        store(second[0], "v")
-        store(second[1], "s")
-        store(third, "v")
+        for part in last:
+            mix(part, 1)
+        store(late[2], "v")
         store(last[0], "s")
         store(last[1], "v")

@@ -30,7 +30,7 @@ def tile_list_ball_cauchy_mix_kernel(tc, tab_words, tab_scales, offs, wk_words, 
         stage = ctx.enter_context(tc.tile_pool(name="stage", bufs=1))
         cast = ctx.enter_context(tc.tile_pool(name="cast", bufs=3))
         hpool = ctx.enter_context(tc.tile_pool(name="hpool", bufs=3))
-        opool = ctx.enter_context(tc.tile_pool(name="opool", bufs=6))
+        opool = ctx.enter_context(tc.tile_pool(name="opool", bufs=9))
         psum = ctx.enter_context(tc.psum_pool(name="psum", bufs=1))
 
         def bank(i, shape):
@@ -53,7 +53,12 @@ def tile_list_ball_cauchy_mix_kernel(tc, tab_words, tab_scales, offs, wk_words, 
             nc.gpsimd.dma_start(bias[e:P:2, :, 0:7], bk.rearrange("(b u k) -> u b k", b=2, k=8)[:, :, e : e + 7])
 
         wk_view = wk_words.rearrange("a p c -> p a c")
-        wkp = [keep.tile([P, 2, PASS // 2], I32, name="wkp%d" % b, align_bytes=64) for b in range(2)]
+        slot = 4 * PACK * HALF
+        wk_bytes = 4 * PASS
+        wkp = [
+            keep.tile([P, 2, PASS // 2], I32, name="wkp0", align_bytes=64),
+            stage.tile([P, 2, PASS // 2], I32, name="wkp1", align_bytes=64, offset=2 * slot),
+        ]
 
         def load_wk(b):
             raw = keep.tile([P, 2, PASS // 2], I32, name="wk_raw", tag="wk_raw", align_bytes=64)
@@ -67,8 +72,6 @@ def tile_list_ball_cauchy_mix_kernel(tc, tab_words, tab_scales, offs, wk_words, 
             )
 
         wk_raw0 = load_wk(0)
-        slot = 4 * PACK * HALF
-        wk_bytes = 4 * PASS
         table = [stage.tile([P, T], I32, name="table%d" % a, align_bytes=64, offset=a * (2 * slot + wk_bytes)) for a in range(2)]
         for a in range(2):
             nc.sync.dma_start(table[a][:], tab_words[a].rearrange("p n t -> p (n t)").bitcast(I32))
@@ -108,7 +111,7 @@ def tile_list_ball_cauchy_mix_kernel(tc, tab_words, tab_scales, offs, wk_words, 
 
         wk_late = stage.tile([P, 2, PASS // 2], I32, name="wk_late", align_bytes=64, offset=slot)
         wk_raw1 = wk_late[:]
-        places = [0, slot + wk_bytes, 2 * slot + wk_bytes, 3 * slot + wk_bytes, 0, slot + wk_bytes]
+        places = [0, slot + wk_bytes, 2 * slot + wk_bytes, 3 * slot + wk_bytes, 0, slot]
         raws = [stage.tile([P, PACK, HALF], F32, name="raw%d" % i, align_bytes=64, offset=places[i]) for i in range(6)]
 
         def raw_slot(i):
@@ -137,8 +140,6 @@ def tile_list_ball_cauchy_mix_kernel(tc, tab_words, tab_scales, offs, wk_words, 
                 in_=raw_slot(2 * b + a).rearrange("p j (u t e) -> p t u j e", t=PACK, e=2),
             )
             grouped["f", a, b] = g
-            if b == 0:
-                load_wm(a)
 
         def quant_wf(a, b):
             codes = keep.tile([P, PASS], U32, name="wfc%d%d" % (a, b), align_bytes=64)
@@ -232,10 +233,10 @@ def tile_list_ball_cauchy_mix_kernel(tc, tab_words, tab_scales, offs, wk_words, 
                     )
 
         def weigh(q, c):
-            if c % 2 == 0:
-                hbs[q, c // 2] = hpool.tile([P, 2, CHUNK * PACK], BF16, name="hb", tag="hb", align_bytes=64)
+            if c == 0:
+                hbs[q] = hpool.tile([P, 4, CHUNK * PACK], BF16, name="hb", tag="hb", align_bytes=64)
             nc.vector.tensor_tensor(
-                out=hbs[q, c // 2][:, c % 2, :].rearrange("p (u i t) -> p u t i", i=2, t=PACK),
+                out=hbs[q][:, c, :].rearrange("p (u i t) -> p u t i", i=2, t=PACK),
                 in0=fs[q, c][:].rearrange("p t (u i) -> p u t i", i=2),
                 in1=ys[q][:, c, :, :].rearrange("p t (u i) -> p u t i", i=2),
                 op=MULT,
@@ -246,7 +247,7 @@ def tile_list_ball_cauchy_mix_kernel(tc, tab_words, tab_scales, offs, wk_words, 
         def quant_h(q, c0, c1):
             b, h = divmod(q, 2)
             tok = slice(h * HALF + c0 * CHUNK, h * HALF + c1 * CHUNK)
-            src = hbs[q, c0 // 2][:, c0 % 2 : c0 % 2 + c1 - c0, :]
+            src = hbs[q][:, c0:c1, :]
             nc.vector.quantize_mx(
                 out=hc[b][:, tok].bitcast(FP8X4), scales=hs[b][:, tok], in_=src.rearrange("p c w -> p (c w)")
             )
@@ -289,7 +290,7 @@ def tile_list_ball_cauchy_mix_kernel(tc, tab_words, tab_scales, offs, wk_words, 
         for t in range(PACK):
             project(0, t, (1, 0), 2, 4, 0, 1)
         cast_wf(0, 0)
-        permute_wk(1, wk_raw1)
+        load_wm(0)
         square(0, 0, 2, 4)
         root(0, 0, 2)
         unroot(0, 0, 2, "v")
@@ -298,43 +299,40 @@ def tile_list_ball_cauchy_mix_kernel(tc, tab_words, tab_scales, offs, wk_words, 
             feature(0, c, (0,))
         for t in range(1, PACK):
             square(0, t, 2, 4)
+        cast_wf(1, 0)
+        permute_wk(1, wk_raw1)
+        load_wm(1)
         square(1, 0)
         root(0, 2, 4)
-        cast_wf(1, 0)
-        unroot(0, 2, 4, "v")
         quant_wf(1, 0)
         for c in range(4):
             feature(0, c, (1,))
+        unroot(0, 2, 4, "v")
         for t in range(1, PACK):
             square(1, t)
         square(2, 0)
-        root(1, 0, 2)
-        root(1, 2, 4)
+        root(1, 0, 4)
         weigh(0, 0)
         weigh(0, 1)
         weigh(0, 2)
-        quant_h(0, 0, 2)
         weigh(0, 3)
         cast_wf(0, 1)
-        quant_h(0, 2, 4)
+        quant_h(0, 0, 4)
         quant_wf(0, 1)
         cast_wf(1, 1)
         for t in range(1, PACK):
             square(2, t)
-        unroot(1, 0, 2, "s")
-        unroot(1, 2, 4, "s")
+        unroot(1, 0, 4, "s")
         quant_wf(1, 1)
         weigh(1, 0)
         weigh(1, 1)
         weigh(1, 2)
-        quant_h(1, 0, 2)
         weigh(1, 3)
-        root(2, 0, 2)
-        root(2, 2, 4)
+        root(2, 0, 4)
         for t in range(PACK):
             square(3, t)
         cast_wm(0)
-        quant_h(1, 2, 4)
+        quant_h(1, 0, 4)
         quant_wm(0)
         cast_wm(1)
         unroot(2, 0, 2, "s")
@@ -356,28 +354,34 @@ def tile_list_ball_cauchy_mix_kernel(tc, tab_words, tab_scales, offs, wk_words, 
         quant_h(2, 2, 4)
         mix(first[2], 1)
         mix(first[3], 1)
-        store(first[1], "v")
-        unroot(3, 0, 2, "s")
-        unroot(3, 2, 3, "s")
-        unroot(3, 3, 4, "s")
-        last = [piece(1, 3, 4, 2 * j, 2 * j + 2, j) for j in range(2)]
-        for part in last:
-            mix(part, 0)
+        for c in range(4):
+            unroot(3, c, c + 1, "s")
+        last = [piece(1, 3, 4, 0, 2, 0)]
+        mix(last[0], 0)
         store(first[2], "s")
         store(first[3], "s")
         weigh(3, 0)
-        late = []
-        for c in range(3):
-            late.append(piece(1, c, c + 1, 0, 4, PACK + c))
-            mix(late[c], 0)
-            weigh(3, c + 1)
-            quant_h(3, c, c + 1)
-            mix(late[c], 1)
-        store(late[0], "s")
-        store(late[1], "s")
+        weigh(3, 1)
+        second = [piece(1, 0, 2, 2 * j, 2 * j + 2, PACK + j) for j in range(2)]
+        for part in second:
+            mix(part, 0)
+        store(first[1], "v")
+        quant_h(3, 0, 2)
+        for part in second:
+            mix(part, 1)
+        last.append(piece(1, 3, 4, 2, 4, 1))
+        mix(last[1], 0)
+        weigh(3, 2)
+        third = piece(1, 2, 3, 0, 4, 6)
+        mix(third, 0)
+        weigh(3, 3)
+        quant_h(3, 2, 3)
+        mix(third, 1)
         quant_h(3, 3, 4)
         for part in last:
             mix(part, 1)
-        store(late[2], "v")
+        store(second[0], "s")
+        store(second[1], "s")
+        store(third, "v")
         store(last[0], "s")
         store(last[1], "v")

@@ -54,10 +54,9 @@ def tile_list_ball_cauchy_mix_kernel(tc, tab_words, tab_scales, offs, wk_words, 
 
         wk_view = wk_words.rearrange("a p c -> p a c")
         slot = 4 * PACK * HALF
-        wk_bytes = 4 * PASS
         wkp = [
             keep.tile([P, 2, PASS // 2], I32, name="wkp0", align_bytes=64),
-            stage.tile([P, 2, PASS // 2], I32, name="wkp1", align_bytes=64, offset=2 * slot),
+            keep.tile([P, 2, PASS // 2], I32, name="wkp1", align_bytes=64),
         ]
 
         def load_wk(b):
@@ -72,32 +71,57 @@ def tile_list_ball_cauchy_mix_kernel(tc, tab_words, tab_scales, offs, wk_words, 
             )
 
         wk_raw0 = load_wk(0)
-        table = [stage.tile([P, T], I32, name="table%d" % a, align_bytes=64, offset=a * (2 * slot + wk_bytes)) for a in range(2)]
-        for a in range(2):
+        table_at = [0, 2 * slot]
+        picked = [
+            stage.tile([P, HALF // 4], I32, name="picked0", align_bytes=64, offset=4 * slot - 64),
+            stage.tile([P, HALF // 4], I32, name="picked1", align_bytes=64, offset=4 * slot),
+        ]
+        table = [stage.tile([P, T], I32, name="table%d" % a, align_bytes=64, offset=table_at[a]) for a in range(2)]
+
+        def load_table(a):
             nc.sync.dma_start(table[a][:], tab_words[a].rearrange("p n t -> p (n t)").bitcast(I32))
+
+        load_table(0)
 
         nc.vector.memset(tscale[32:64, :], 0)
         nc.vector.memset(tscale[64:128, :], 0)
         nc.vector.memset(kscale_raw[32:64, :], 0)
         nc.vector.memset(kscale_raw[64:128, :], 0)
-        planes = [keep.tile([P, (S + H) // 4], I32, name="plane%d" % a, align_bytes=64) for a in range(2)]
-        for a in range(2):
-            nc.vector.memset(planes[a][:], 0)
+        planes = [
+            [keep.tile([P, (HALF + PASS) // 4], I32, name="plane%d%d" % (g, a), align_bytes=64) for a in range(2)]
+            for g in range(2)
+        ]
 
-        picked = keep.tile([P, S // 4], I32, name="picked", align_bytes=64)
-        nc.vector.tensor_copy(picked[:].bitcast(U8), tscale[:].bitcast(U8).indirect(offsets[:]))
-        rows = keep.tile([P, (S + H) // 4], I32, name="rows", align_bytes=64)
-        nc.vector.tensor_copy(
-            out=rows[:, S // 4 :].bitcast(U16).rearrange("p (b t u) -> p b t u", b=2, t=PACK),
-            in_=kscale_raw[:].bitcast(U16).rearrange("p (b u t) -> p b t u", b=2, t=PACK),
-        )
-        nc.vector.tensor_copy(rows[0:32, 0 : S // 4], picked[0:32, :])
+        def make_planes(g, queue):
+            rows = stage.tile([P, (HALF + PASS) // 4], I32, name="rows%d" % g, align_bytes=64, offset=5 * slot + HALF - 64 * (1 - g))
+            nc.vector.memset(planes[g][1][:], 0)
+            for dst in (planes[g][0], rows):
+                nc.vector.tensor_copy(
+                    out=dst[:, HALF // 4 :].bitcast(U16).rearrange("p (t u) -> p t u", t=PACK),
+                    in_=kscale_raw[:, g * PASS // 4 : (g + 1) * PASS // 4].bitcast(U16).rearrange("p (u t) -> p t u", t=PACK),
+                )
+            nc.vector.tensor_copy(
+                picked[g][:].bitcast(U8),
+                tscale[:].bitcast(U8).indirect(offsets[:, g * HALF // 16 : (g + 1) * HALF // 16]),
+            )
+            nc.vector.tensor_copy(planes[g][0][:, 0 : HALF // 4], picked[g][:])
+            nc.gpsimd.dma_start(planes[g][1][96:100, :], planes[g][0][28:32, :])
+            nc.vector.tensor_copy(rows[0:32, 0 : HALF // 4], picked[g][0:32, :])
+            for row in range(4, 28, 4):
+                a, q = divmod(row // 4, 4)
+                queue.dma_start(planes[g][a][32 * q : 32 * q + 4, :], rows[row : row + 4, :])
+
+        make_planes(0, nc.sync)
+        load_table(1)
+        make_planes(1, nc.scalar)
         permute_wk(0, wk_raw0[:])
-        nc.vector.tensor_copy(planes[0][0:32, :], rows[0:32, :])
-        for row in range(4, 32, 4):
-            a, q = divmod(row // 4, 4)
-            queue = nc.gpsimd if row == 28 else nc.scalar
-            queue.dma_start(planes[a][32 * q : 32 * q + 4, :], rows[row : row + 4, :])
+
+        def token_scales(a, tok):
+            g, j0 = divmod(tok.start, HALF)
+            return planes[g][a][:].bitcast(U8)[:, j0 : j0 + tok.stop - tok.start]
+
+        def wk_scale(a, b, t):
+            return planes[b][a][:].bitcast(U8)[:, HALF + t * P : HALF + (t + 1) * P]
 
         vw = [keep.tile([P, S], I32, name="vw%d" % a, align_bytes=64) for a in range(2)]
         cuts = [(0, HALF, S), (0, HALF // 2, HALF, S)]
@@ -107,11 +131,10 @@ def tile_list_ball_cauchy_mix_kernel(tc, tab_words, tab_scales, offs, wk_words, 
                     vw[a][:, j0:j1].bitcast(U32),
                     table[a][:].bitcast(U32).indirect(offsets[:, j0 // 16 : j1 // 16]),
                 )
-        planes8 = [planes[a][:].bitcast(U8) for a in range(2)]
 
         wk_late = stage.tile([P, 2, PASS // 2], I32, name="wk_late", align_bytes=64, offset=slot)
         wk_raw1 = wk_late[:]
-        places = [0, slot + wk_bytes, 2 * slot + wk_bytes, 3 * slot + wk_bytes, 0, slot]
+        places = [4 * slot + HALF, 0, 2 * slot, 3 * slot, 4 * slot + HALF, 0]
         raws = [stage.tile([P, PACK, HALF], F32, name="raw%d" % i, align_bytes=64, offset=places[i]) for i in range(6)]
 
         def raw_slot(i):
@@ -172,13 +195,12 @@ def tile_list_ball_cauchy_mix_kernel(tc, tab_words, tab_scales, offs, wk_words, 
             if (q, t, c0) not in xs:
                 xs[q, t, c0] = bank(first_bank + t, [P, (c1 - c0) * CHUNK])
             for a in passes:
-                k0 = S + b * PASS + t * P
                 nc.tensor.matmul_mx(
                     out=xs[q, t, c0][:],
                     lhsT=wkp[b][:, a, t * P // 2 : (t + 1) * P // 2].bitcast(U8).bitcast(FP4X4),
-                    lhsT_scale=planes8[a][:, k0 : k0 + P],
+                    lhsT_scale=wk_scale(a, b, t),
                     rhs=vw[a][:, tok].bitcast(FP8X4),
-                    rhs_scale=planes8[a][:, tok],
+                    rhs_scale=token_scales(a, tok),
                     start=(a == first),
                     stop=(a != first),
                 )
@@ -227,7 +249,7 @@ def tile_list_ball_cauchy_mix_kernel(tc, tab_words, tab_scales, offs, wk_words, 
                         lhsT=codes[:, t * P : (t + 1) * P].bitcast(FP8X4),
                         lhsT_scale=scales[:, t * P : (t + 1) * P],
                         rhs=vw[a][:, tok].bitcast(FP8X4),
-                        rhs_scale=planes8[a][:, tok],
+                        rhs_scale=token_scales(a, tok),
                         start=(a == 0 and t == 0),
                         stop=(a == 1 and t == PACK - 1),
                     )
@@ -285,10 +307,12 @@ def tile_list_ball_cauchy_mix_kernel(tc, tab_words, tab_scales, offs, wk_words, 
         for t in range(PACK):
             project(0, t, (0,), 0, 2, PACK)
         for t in range(PACK):
+            project(0, t, (0,), 2, 4, 0)
+        for t in range(PACK):
             project(0, t, (1,), 0, 2, PACK)
             square(0, t, 0, 2)
         for t in range(PACK):
-            project(0, t, (1, 0), 2, 4, 0, 1)
+            project(0, t, (1,), 2, 4, 0)
         cast_wf(0, 0)
         load_wm(0)
         square(0, 0, 2, 4)

@@ -15,12 +15,18 @@ FP8X4 = mybir.dt.float8_e4m3fn_x4
 FP4X4 = mybir.dt.float4_e2m1fn_x4
 ACT = mybir.ActivationFunctionType
 MULT = mybir.AluOpType.mult
+ADD = mybir.AluOpType.add
 
 P = 128
 PACK = 4
 PASS = P * PACK
 HALF = 512
 CHUNK = 128
+WIDE = PACK * HALF
+KB = 1024
+EDGE = 64
+POOL_COLS = 896
+POOL_CAST = 320
 
 
 def tile_list_ball_cauchy_mix_kernel(tc, tab_words, tab_scales, offs, wk_words, wk_scales, bk, wf, wm, out):
@@ -28,170 +34,187 @@ def tile_list_ball_cauchy_mix_kernel(tc, tab_words, tab_scales, offs, wk_words, 
     with ExitStack() as ctx:
         keep = ctx.enter_context(tc.tile_pool(name="keep", bufs=1))
         stage = ctx.enter_context(tc.tile_pool(name="stage", bufs=1))
-        cast = ctx.enter_context(tc.tile_pool(name="cast", bufs=3))
-        hpool = ctx.enter_context(tc.tile_pool(name="hpool", bufs=3))
         opool = ctx.enter_context(tc.tile_pool(name="opool", bufs=9))
         psum = ctx.enter_context(tc.psum_pool(name="psum", bufs=1))
 
         def bank(i, shape):
             return psum.tile(shape, F32, name="bank%d" % i, tag="bank%d" % i)
 
+        def placed(name, shape, dtype, at):
+            return stage.tile(shape, dtype, name=name, align_bytes=EDGE, offset=at)
+
+        at_table = [0, 16 * KB]
+        at_picked = [32 * KB - EDGE, 32 * KB]
+        at_rows = [35 * KB, 12 * KB]
+        at_wk_late = at_rows[0] + EDGE - 2 * KB
+        at_raw_first = at_rows[0] + HALF + H - EDGE
+        at_raw = [at_raw_first, 0, 16 * KB, 24 * KB, at_raw_first, 0]
+        at_root0 = 45 * KB
+        at_root3 = at_raw[2]
+        at_rounded = [57 * KB, at_root0 + 8 * KB, 61 * KB, 57 * KB, 61 * KB, at_raw[4]]
+        at_gate = [None, at_rounded[1] + EDGE - 8 * KB, None, at_rounded[5] + EDGE - 8 * KB]
+        at_h = [8 * KB, at_raw[4] + 4 * KB, at_rounded[5] + EDGE]
+
         offsets = keep.tile([P, S // 16], U16, name="offsets")
         nc.sync.dma_start(offsets[:], offs)
 
-        tscale = keep.tile([P, T // 4], I32, name="tscale", align_bytes=64)
+        tscale = keep.tile([P, T // 4], I32, name="tscale", align_bytes=EDGE)
         nc.sync.dma_start(tscale[0:32, :], tab_scales.rearrange("a q c -> (a q) c").bitcast(I32))
-        kscale_raw = keep.tile([P, H // 4], I32, name="kscale_raw", align_bytes=64)
-        nc.sync.dma_start(kscale_raw[0:32, :], wk_scales.rearrange("a q c -> (a q) c").bitcast(I32))
+        kscale = keep.tile([P, H // 4], I32, name="kscale", align_bytes=EDGE)
+        nc.sync.dma_start(kscale[0:32, :], wk_scales.rearrange("a q c -> (a q) c").bitcast(I32))
 
         warm = keep.tile([P, 2], F32, name="warm")
         nc.gpsimd.memset(warm[:, 0:1], 1.0)
         nc.scalar.activation(out=warm[:, 1:2], in_=warm[:, 0:1], func=ACT.Abs_reciprocal_sqrt)
 
-        bias = keep.tile([P, 2, 8], F32, name="bias", align_bytes=64)
+        bias = keep.tile([P, 2, 8], F32, name="bias", align_bytes=EDGE)
         for e in range(2):
             nc.gpsimd.dma_start(bias[e:P:2, :, 0:7], bk.rearrange("(b u k) -> u b k", b=2, k=8)[:, :, e : e + 7])
 
         wk_view = wk_words.rearrange("a p c -> p a c")
-        slot = 4 * PACK * HALF
-        wkp = [
-            keep.tile([P, 2, PASS // 2], I32, name="wkp0", align_bytes=64),
-            keep.tile([P, 2, PASS // 2], I32, name="wkp1", align_bytes=64),
+        wk_raw = [
+            keep.tile([P, 2, PASS // 2], I32, name="wk_raw0", align_bytes=EDGE),
+            placed("wk_raw1", [P, 2, PASS // 2], I32, at_wk_late),
         ]
+        wkp = [keep.tile([P, 2, PASS // 2], I32, name="wkp%d" % b, align_bytes=EDGE) for b in range(2)]
 
         def load_wk(b):
-            raw = keep.tile([P, 2, PASS // 2], I32, name="wk_raw", tag="wk_raw", align_bytes=64)
-            nc.sync.dma_start(raw[:], wk_view[:, :, 2 * PASS * b : 2 * PASS * (b + 1)].bitcast(I32))
-            return raw
+            nc.sync.dma_start(wk_raw[b][:], wk_view[:, :, 2 * PASS * b : 2 * PASS * (b + 1)].bitcast(I32))
 
-        def permute_wk(b, raw):
+        def permute_wk(b):
             nc.vector.tensor_copy(
                 out=wkp[b][:].rearrange("p a (t v w) -> p a v t w", t=PACK, w=4),
-                in_=raw.rearrange("p a (v w t) -> p a v t w", t=PACK, w=4),
+                in_=wk_raw[b][:].rearrange("p a (v w t) -> p a v t w", t=PACK, w=4),
             )
 
-        wk_raw0 = load_wk(0)
-        table_at = [0, 2 * slot]
-        picked = [
-            stage.tile([P, HALF // 4], I32, name="picked0", align_bytes=64, offset=4 * slot - 64),
-            stage.tile([P, HALF // 4], I32, name="picked1", align_bytes=64, offset=4 * slot),
-        ]
-        table = [stage.tile([P, T], I32, name="table%d" % a, align_bytes=64, offset=table_at[a]) for a in range(2)]
+        picked = [placed("picked%d" % h, [P, HALF // 4], I32, at_picked[h]) for h in range(2)]
+        table = [placed("table%d" % a, [P, T], I32, at_table[a]) for a in range(2)]
 
         def load_table(a):
             nc.sync.dma_start(table[a][:], tab_words[a].rearrange("p n t -> p (n t)").bitcast(I32))
 
+        load_wk(0)
         load_table(0)
 
         nc.vector.memset(tscale[32:64, :], 0)
         nc.vector.memset(tscale[64:128, :], 0)
-        nc.vector.memset(kscale_raw[32:64, :], 0)
-        nc.vector.memset(kscale_raw[64:128, :], 0)
+        nc.vector.memset(kscale[32:64, :], 0)
+        nc.vector.memset(kscale[64:128, :], 0)
+        widths = [(HALF + H) // 4, HALF // 4]
         planes = [
-            [keep.tile([P, (HALF + PASS) // 4], I32, name="plane%d%d" % (g, a), align_bytes=64) for a in range(2)]
-            for g in range(2)
+            [keep.tile([P, widths[h]], I32, name="plane%d%d" % (h, a), align_bytes=EDGE) for a in range(2)]
+            for h in range(2)
         ]
 
-        def make_planes(g, queue):
-            rows = stage.tile([P, (HALF + PASS) // 4], I32, name="rows%d" % g, align_bytes=64, offset=5 * slot + HALF - 64 * (1 - g))
-            nc.vector.memset(planes[g][1][:], 0)
-            for dst in (planes[g][0], rows):
-                nc.vector.tensor_copy(
-                    out=dst[:, HALF // 4 :].bitcast(U16).rearrange("p (t u) -> p t u", t=PACK),
-                    in_=kscale_raw[:, g * PASS // 4 : (g + 1) * PASS // 4].bitcast(U16).rearrange("p (u t) -> p t u", t=PACK),
-                )
+        def reorder_wk_scales(dst):
             nc.vector.tensor_copy(
-                picked[g][:].bitcast(U8),
-                tscale[:].bitcast(U8).indirect(offsets[:, g * HALF // 16 : (g + 1) * HALF // 16]),
+                out=dst[:, HALF // 4 :].bitcast(U16).rearrange("p (b t u) -> p b t u", b=2, t=PACK),
+                in_=kscale[:].bitcast(U16).rearrange("p (b u t) -> p b t u", b=2, t=PACK),
             )
-            nc.vector.tensor_copy(planes[g][0][:, 0 : HALF // 4], picked[g][:])
-            nc.gpsimd.dma_start(planes[g][1][96:100, :], planes[g][0][28:32, :])
-            nc.vector.tensor_copy(rows[0:32, 0 : HALF // 4], picked[g][0:32, :])
+
+        def pick_scales(h):
+            nc.vector.memset(planes[h][1][:], 0)
+            nc.vector.tensor_copy(
+                picked[h][:].bitcast(U8),
+                tscale[:].bitcast(U8).indirect(offsets[:, h * HALF // 16 : (h + 1) * HALF // 16]),
+            )
+            nc.vector.tensor_copy(planes[h][0][:, 0 : HALF // 4], picked[h][:])
+            nc.gpsimd.dma_start(planes[h][1][96:100, :], planes[h][0][28:32, :])
+
+        def move_scales(h):
+            rows = placed("rows%d" % h, [P, widths[h]], I32, at_rows[h])
+            if h == 0:
+                reorder_wk_scales(rows)
+            nc.vector.tensor_copy(rows[0:32, 0 : HALF // 4], picked[h][0:32, :])
             for row in range(4, 28, 4):
                 a, q = divmod(row // 4, 4)
-                queue.dma_start(planes[g][a][32 * q : 32 * q + 4, :], rows[row : row + 4, :])
+                nc.sync.dma_start(planes[h][a][32 * q : 32 * q + 4, :], rows[row : row + 4, :])
 
-        make_planes(0, nc.sync)
+        reorder_wk_scales(planes[0][0])
+        pick_scales(0)
+        move_scales(0)
         load_table(1)
-        make_planes(1, nc.scalar)
-        permute_wk(0, wk_raw0[:])
+        pick_scales(1)
+        permute_wk(0)
 
-        def token_scales(a, tok):
-            g, j0 = divmod(tok.start, HALF)
-            return planes[g][a][:].bitcast(U8)[:, j0 : j0 + tok.stop - tok.start]
+        def token_scales(a, h, c0, c1):
+            return planes[h][a][:].bitcast(U8)[:, c0 * CHUNK : c1 * CHUNK]
 
         def wk_scale(a, b, t):
-            return planes[b][a][:].bitcast(U8)[:, HALF + t * P : HALF + (t + 1) * P]
+            k0 = HALF + b * PASS + t * P
+            return planes[0][a][:].bitcast(U8)[:, k0 : k0 + P]
 
-        vw = [keep.tile([P, S], I32, name="vw%d" % a, align_bytes=64) for a in range(2)]
-        cuts = [(0, HALF, S), (0, HALF // 2, HALF, S)]
-        for a in range(2):
-            for j0, j1 in zip(cuts[a], cuts[a][1:]):
-                nc.vector.tensor_copy(
-                    vw[a][:, j0:j1].bitcast(U32),
-                    table[a][:].bitcast(U32).indirect(offsets[:, j0 // 16 : j1 // 16]),
-                )
+        vw = [keep.tile([P, S], I32, name="vw%d" % a, align_bytes=EDGE) for a in range(2)]
 
-        wk_late = stage.tile([P, 2, PASS // 2], I32, name="wk_late", align_bytes=64, offset=slot)
-        wk_raw1 = wk_late[:]
-        places = [4 * slot + HALF, 0, 2 * slot, 3 * slot, 4 * slot + HALF, 0]
-        raws = [stage.tile([P, PACK, HALF], F32, name="raw%d" % i, align_bytes=64, offset=places[i]) for i in range(6)]
+        def gather(a, j0, j1):
+            nc.vector.tensor_copy(
+                vw[a][:, j0:j1].bitcast(U32),
+                table[a][:].bitcast(U32).indirect(offsets[:, j0 // 16 : j1 // 16]),
+            )
 
-        def raw_slot(i):
-            return raws[i][:]
+        def tokens(a, h, c0, c1):
+            return vw[a][:, h * HALF + c0 * CHUNK : h * HALF + c1 * CHUNK].bitcast(FP8X4)
 
-        for b in range(2):
-            for a in range(2):
-                src = wf[a * PASS : (a + 1) * PASS, b * PASS : (b + 1) * PASS]
-                nc.sync.dma_start(raw_slot(2 * b + a), src.rearrange("(p j) c -> p j c", j=PACK))
-                if (a, b) == (1, 0):
-                    nc.sync.dma_start(wk_raw1, wk_view[:, :, 2 * PASS : 4 * PASS].bitcast(I32))
+        raws = [placed("raw%d" % i, [P, PACK, HALF], F32, at_raw[i]) for i in range(6)]
+        rounded = {}
+        quantised = {}
+
+        def load_wf(i):
+            b, a = divmod(i, 2)
+            src = wf[a * PASS : (a + 1) * PASS, b * PASS : (b + 1) * PASS]
+            nc.sync.dma_start(raws[i][:], src.rearrange("(p j) c -> p j c", j=PACK))
 
         def load_wm(b):
             src = wm[b * PASS : (b + 1) * PASS, :].rearrange("(u t e) c -> e u t c", t=PACK, e=2)
             for e in range(2):
-                nc.sync.dma_start(raw_slot(4 + b)[e:P:2], src[e])
+                nc.sync.dma_start(raws[4 + b][e:P:2], src[e])
 
-        wfq = {}
-        wmq = {}
-        grouped = {}
+        def cast(i):
+            rounded[i] = placed("rounded%d" % i, [P, WIDE], BF16, at_rounded[i])
+            if i < 4:
+                nc.vector.tensor_copy(
+                    out=rounded[i][:].rearrange("p (t u e j) -> p t u j e", t=PACK, e=2, j=PACK),
+                    in_=raws[i][:].rearrange("p j (u t e) -> p t u j e", t=PACK, e=2),
+                )
+            else:
+                nc.vector.tensor_copy(
+                    out=rounded[i][:].rearrange("p (c i j) -> p c j i", i=2, j=PACK),
+                    in_=raws[i][:].rearrange("p j (c i) -> p c j i", i=2),
+                )
 
-        def cast_wf(a, b):
-            g = cast.tile([P, PACK * PASS], BF16, name="grouped", tag="grouped", align_bytes=64)
-            nc.vector.tensor_copy(
-                out=g[:].rearrange("p (t u e j) -> p t u j e", t=PACK, e=2, j=PACK),
-                in_=raw_slot(2 * b + a).rearrange("p j (u t e) -> p t u j e", t=PACK, e=2),
+        def cast_wm_pool(i):
+            rounded[i] = placed("rounded%d" % i, [P, WIDE], BF16, at_rounded[i])
+            nc.gpsimd.tensor_scalar(
+                out=rounded[i][:, 0 : POOL_CAST * PACK].rearrange("p (c j) -> p c j", j=PACK),
+                in0=raws[i][:, :, 0:POOL_CAST].rearrange("p j c -> p c j"),
+                scalar1=1.0,
+                scalar2=0.0,
+                op0=MULT,
+                op1=ADD,
             )
-            grouped["f", a, b] = g
 
-        def quant_wf(a, b):
-            codes = keep.tile([P, PASS], U32, name="wfc%d%d" % (a, b), align_bytes=64)
-            scales = keep.tile([P, PASS], U8, name="wfs%d%d" % (a, b), align_bytes=64)
-            nc.vector.quantize_mx(out=codes[:].bitcast(FP8X4), scales=scales[:], in_=grouped["f", a, b][:])
-            wfq[a, b] = (codes, scales)
-
-        def cast_wm(b):
-            g = cast.tile([P, PACK * N], BF16, name="grouped", tag="grouped", align_bytes=64)
+        def cast_wm_rest(i):
             nc.vector.tensor_copy(
-                out=g[:].rearrange("p (c i j) -> p c j i", i=2, j=PACK),
-                in_=raw_slot(4 + b).rearrange("p j (c i) -> p c j i", i=2),
+                out=rounded[i][:, POOL_CAST * PACK :].rearrange("p (c i j) -> p c j i", i=2, j=PACK),
+                in_=raws[i][:, :, POOL_CAST:].rearrange("p j (c i) -> p c j i", i=2),
             )
-            grouped["m", b] = g
 
-        def quant_wm(b):
-            codes = keep.tile([P, N], U32, name="wmc%d" % b, align_bytes=64)
-            scales = keep.tile([P, N], U8, name="wms%d" % b, align_bytes=64)
-            nc.vector.quantize_mx(out=codes[:].bitcast(FP8X4), scales=scales[:], in_=grouped["m", b][:])
-            wmq[b] = (codes, scales)
+        def quant_w(i):
+            codes = keep.tile([P, PASS], U32, name="wcodes%d" % i, align_bytes=EDGE)
+            scales = keep.tile([P, PASS], U8, name="wscales%d" % i, align_bytes=EDGE)
+            nc.vector.quantize_mx(out=codes[:].bitcast(FP8X4), scales=scales[:], in_=rounded[i][:])
+            quantised[i] = (codes, scales)
 
-        ys = [keep.tile([P, HALF // CHUNK, PACK, CHUNK], F32, name="y%d" % q) for q in range(4)]
+        ys = [keep.tile([P, WIDE], F32, name="y%d" % q) for q in range(4)]
+        roots = [placed("root0", [P, WIDE], F32, at_root0)]
+        roots = roots + [keep.tile([P, WIDE], F32, name="root%d" % q) for q in range(1, 3)]
+        roots = roots + [placed("root3", [P, WIDE], F32, at_root3)]
+        gates = [ys[q] if q % 2 == 0 else placed("gate%d" % q, [P, WIDE], F32, at_gate[q]) for q in range(4)]
         xs = {}
         fs = {}
-        hbs = {}
 
-        def project(q, t, passes, c0=0, c1=4, first_bank=0, first=0):
-            b, h = divmod(q, 2)
-            tok = slice(h * HALF + c0 * CHUNK, h * HALF + c1 * CHUNK)
+        def project(q, t, passes, c0=0, c1=4, first_bank=0):
+            h, b = divmod(q, 2)
             if (q, t, c0) not in xs:
                 xs[q, t, c0] = bank(first_bank + t, [P, (c1 - c0) * CHUNK])
             for a in passes:
@@ -199,110 +222,132 @@ def tile_list_ball_cauchy_mix_kernel(tc, tab_words, tab_scales, offs, wk_words, 
                     out=xs[q, t, c0][:],
                     lhsT=wkp[b][:, a, t * P // 2 : (t + 1) * P // 2].bitcast(U8).bitcast(FP4X4),
                     lhsT_scale=wk_scale(a, b, t),
-                    rhs=vw[a][:, tok].bitcast(FP8X4),
-                    rhs_scale=token_scales(a, tok),
-                    start=(a == first),
-                    stop=(a != first),
+                    rhs=tokens(a, h, c0, c1),
+                    rhs_scale=token_scales(a, h, c0, c1),
+                    start=(a == 0),
+                    stop=(a == 1),
                 )
+
+        def chunks(tile, c0, c1):
+            return tile[:].rearrange("p (t j) -> p t j", t=PACK)[:, :, c0 * CHUNK : c1 * CHUNK]
 
         def square(q, t, c0=0, c1=4):
             nc.scalar.activation(
-                out=ys[q][:, c0:c1, t, :],
-                in_=xs[q, t, c0][:].rearrange("p (c n) -> p c n", n=CHUNK),
+                out=chunks(ys[q], c0, c1)[:, t, :],
+                in_=xs[q, t, c0][:],
                 func=ACT.Square,
-                bias=bias[:, q // 2, 2 * t : 2 * t + 1],
+                bias=bias[:, q % 2, 2 * t : 2 * t + 1],
             )
-            if q <= 2 and c1 == 4:
+            if q <= 1 and c1 == 4:
                 project(q + 1, t, (0, 1))
 
-        roots = [keep.tile([P, HALF * PACK], F32, name="root%d" % q) for q in range(4)]
+        def root(q, view):
+            nc.scalar.activation(out=view(roots[q]), in_=view(ys[q]), func=ACT.Abs_reciprocal_sqrt, bias=1.0)
 
-        def gate(q, c0, c1):
-            return ys[q][:, c0:c1, :, :].rearrange("p c t n -> p (c t n)")
-
-        def root(q, c0, c1):
-            part = roots[q][:, c0 * PASS : c1 * PASS]
-            nc.scalar.activation(out=part, in_=gate(q, c0, c1), func=ACT.Abs_reciprocal_sqrt, bias=1.0)
-
-        def unroot(q, c0, c1, eng):
-            part = roots[q][:, c0 * PASS : c1 * PASS]
-            if eng == "s":
-                nc.scalar.activation(out=gate(q, c0, c1), in_=part, func=ACT.Square)
-            elif eng == "v":
-                nc.vector.tensor_tensor(out=gate(q, c0, c1), in0=part, in1=part, op=MULT)
+        def unroot(q, view, eng):
+            if eng is nc.scalar:
+                nc.scalar.activation(out=view(gates[q]), in_=view(roots[q]), func=ACT.Square)
             else:
-                nc.gpsimd.tensor_tensor(out=gate(q, c0, c1), in0=part, in1=part, op=MULT)
+                eng.tensor_tensor(out=view(gates[q]), in0=view(roots[q]), in1=view(roots[q]), op=MULT)
 
-        hc = [keep.tile([P, S], U32, name="hc%d" % b, align_bytes=64) for b in range(2)]
-        hs = [keep.tile([P, S], U8, name="hs%d" % b, align_bytes=64) for b in range(2)]
+        def of_chunks(c0, c1):
+            return lambda tile: chunks(tile, c0, c1)
 
-        def feature(q, c, passes=(0, 1)):
-            b, h = divmod(q, 2)
-            tok = slice(h * HALF + c * CHUNK, h * HALF + (c + 1) * CHUNK)
+        def of_columns(lo, hi):
+            return lambda tile: tile[:, lo:hi]
+
+        def feature(q, c, i, passes=(0, 1)):
+            h, b = divmod(q, 2)
             if (q, c) not in fs:
-                fs[q, c] = bank(PACK + c, [P, PACK, CHUNK])
+                fs[q, c] = bank(i, [P, PACK, CHUNK])
             for a in passes:
-                codes, scales = wfq[a, b]
+                codes, scales = quantised[2 * b + a]
                 for t in range(PACK):
                     nc.tensor.matmul_mx(
                         out=fs[q, c][:, t, :],
                         lhsT=codes[:, t * P : (t + 1) * P].bitcast(FP8X4),
                         lhsT_scale=scales[:, t * P : (t + 1) * P],
-                        rhs=vw[a][:, tok].bitcast(FP8X4),
-                        rhs_scale=token_scales(a, tok),
+                        rhs=tokens(a, h, c, c + 1),
+                        rhs_scale=token_scales(a, h, c, c + 1),
                         start=(a == 0 and t == 0),
                         stop=(a == 1 and t == PACK - 1),
                     )
 
+        hb = {}
+        hcodes = [
+            placed("hcodes2", [P, HALF], U32, at_root3) if q == 2 else keep.tile([P, HALF], U32, name="hcodes%d" % q, align_bytes=EDGE)
+            for q in range(4)
+        ]
+
+        def h_codes(s0, s1):
+            return hcodes[s0 // 4][:, (s0 % 4) * CHUNK : (s0 % 4 + s1 - s0) * CHUNK].bitcast(FP8X4)
+
+        hscales = keep.tile([P, 16 * CHUNK], U8, name="hscales", align_bytes=EDGE)
+
+        def h_slots(s0, s1):
+            g = min(s0 // 4, 2)
+            if g not in hb:
+                hb[g] = placed("h%d" % g, [P, (1 + g // 2) * WIDE], BF16, at_h[g])
+            return hb[g][:, (s0 - 4 * g) * PASS : (s1 - 4 * g) * PASS]
+
         def weigh(q, c):
-            if c == 0:
-                hbs[q] = hpool.tile([P, 4, CHUNK * PACK], BF16, name="hb", tag="hb", align_bytes=64)
+            s0 = 4 * q + c
             nc.vector.tensor_tensor(
-                out=hbs[q][:, c, :].rearrange("p (u i t) -> p u t i", i=2, t=PACK),
+                out=h_slots(s0, s0 + 1).rearrange("p (u i t) -> p u t i", i=2, t=PACK),
                 in0=fs[q, c][:].rearrange("p t (u i) -> p u t i", i=2),
-                in1=ys[q][:, c, :, :].rearrange("p t (u i) -> p u t i", i=2),
+                in1=chunks(gates[q], c, c + 1).rearrange("p t (u i) -> p u t i", i=2),
                 op=MULT,
             )
-            if q <= 2:
-                feature(q + 1, c)
 
-        def quant_h(q, c0, c1):
-            b, h = divmod(q, 2)
-            tok = slice(h * HALF + c0 * CHUNK, h * HALF + c1 * CHUNK)
-            src = hbs[q][:, c0:c1, :]
+        def quant_h(s0, s1):
             nc.vector.quantize_mx(
-                out=hc[b][:, tok].bitcast(FP8X4), scales=hs[b][:, tok], in_=src.rearrange("p c w -> p (c w)")
+                out=h_codes(s0, s1),
+                scales=hscales[:, s0 * CHUNK : s1 * CHUNK],
+                in_=h_slots(s0, s1),
             )
 
         out_view = out.rearrange("(g p) s -> p g s", p=P)
 
         def piece(h, c0, c1, g0, g1, i):
-            tok = slice(h * HALF + c0 * CHUNK, h * HALF + c1 * CHUNK)
-            return bank(i, [P, g1 - g0, (c1 - c0) * CHUNK]), tok, g0, g1
+            return bank(i, [P, g1 - g0, (c1 - c0) * CHUNK]), h, c0, c1, g0, g1
 
         def mix(part, b):
-            acc, tok, g0, g1 = part
-            codes, scales = wmq[b]
+            acc, h, c0, c1, g0, g1 = part
+            codes, scales = quantised[4 + b]
+            s0 = 4 * (2 * h + b) + c0
+            cols = slice(s0 * CHUNK, (s0 + c1 - c0) * CHUNK)
             for g in range(g0, g1):
                 nc.tensor.matmul_mx(
                     out=acc[:, g - g0, :],
                     lhsT=codes[:, g * P : (g + 1) * P].bitcast(FP8X4),
                     lhsT_scale=scales[:, g * P : (g + 1) * P],
-                    rhs=hc[b][:, tok].bitcast(FP8X4),
-                    rhs_scale=hs[b][:, tok],
+                    rhs=h_codes(s0, s0 + c1 - c0),
+                    rhs_scale=hscales[:, cols],
                     start=(b == 0 and g == g0),
                     stop=(b == 1 and g == g1 - 1),
                 )
 
-        def store(mixed, eng):
-            acc, tok, g0, g1 = mixed
-            dst = out_view[:, g0:g1, tok]
+        def store(part, eng):
+            acc, h, c0, c1, g0, g1 = part
             res = opool.tile(list(acc.shape), F32, name="res", tag="res")
-            if eng == "v":
+            if eng is nc.vector:
                 nc.vector.tensor_copy(out=res[:], in_=acc[:])
             else:
                 nc.scalar.copy(out=res[:], in_=acc[:])
-            nc.sync.dma_start(dst, res[:])
+            nc.sync.dma_start(out_view[:, g0:g1, h * HALF + c0 * CHUNK : h * HALF + c1 * CHUNK], res[:])
+
+        gather(0, 0, HALF)
+        gather(0, HALF, S)
+        load_wk(1)
+        load_wf(0)
+        load_wf(1)
+        move_scales(1)
+        load_wf(2)
+        load_wf(3)
+        gather(1, 0, HALF // 2)
+        gather(1, HALF // 2, HALF)
+        permute_wk(1)
+        gather(1, HALF, S)
 
         for t in range(PACK):
             project(0, t, (0,), 0, 2, PACK)
@@ -313,99 +358,113 @@ def tile_list_ball_cauchy_mix_kernel(tc, tab_words, tab_scales, offs, wk_words, 
             square(0, t, 0, 2)
         for t in range(PACK):
             project(0, t, (1,), 2, 4, 0)
-        cast_wf(0, 0)
+
+        cast(0)
         load_wm(0)
         square(0, 0, 2, 4)
-        root(0, 0, 2)
-        unroot(0, 0, 2, "v")
-        quant_wf(0, 0)
+        root(0, of_chunks(0, 2))
+        unroot(0, of_chunks(0, 2), nc.vector)
+        quant_w(0)
         for c in range(4):
-            feature(0, c, (0,))
+            feature(0, c, PACK + c, (0,))
         for t in range(1, PACK):
             square(0, t, 2, 4)
-        cast_wf(1, 0)
-        permute_wk(1, wk_raw1)
+        cast(1)
         load_wm(1)
         square(1, 0)
-        root(0, 2, 4)
-        quant_wf(1, 0)
+        root(0, of_chunks(2, 4))
+        unroot(0, of_chunks(2, 3), nc.vector)
+        quant_w(1)
         for c in range(4):
-            feature(0, c, (1,))
-        unroot(0, 2, 4, "v")
-        for t in range(1, PACK):
-            square(1, t)
-        square(2, 0)
-        root(1, 0, 4)
-        weigh(0, 0)
-        weigh(0, 1)
-        weigh(0, 2)
-        weigh(0, 3)
-        cast_wf(0, 1)
-        quant_h(0, 0, 4)
-        quant_wf(0, 1)
-        cast_wf(1, 1)
-        for t in range(1, PACK):
-            square(2, t)
-        unroot(1, 0, 4, "s")
-        quant_wf(1, 1)
-        weigh(1, 0)
-        weigh(1, 1)
-        weigh(1, 2)
-        weigh(1, 3)
-        root(2, 0, 4)
-        for t in range(PACK):
-            square(3, t)
-        cast_wm(0)
-        quant_h(1, 0, 4)
-        quant_wm(0)
-        cast_wm(1)
-        unroot(2, 0, 2, "s")
-        unroot(2, 2, 4, "s")
-        first = [piece(0, 2 * (i // 2), 2 * (i // 2) + 2, 2 * (i % 2), 2 * (i % 2) + 2, i) for i in range(4)]
+            feature(0, c, PACK + c, (1,))
+        unroot(0, of_chunks(3, 4), nc.vector)
+
+        pooled = of_columns(0, POOL_COLS)
+        rest = of_columns(POOL_COLS, WIDE)
+        whole = of_columns(0, WIDE)
+
+        def start_roots(q):
+            square(q, 2)
+            root(q, pooled)
+            square(q, 3)
+
+        def finish_gates(q):
+            square(q + 1, 0)
+            root(q, rest)
+            square(q + 1, 1)
+            unroot(q, rest, nc.scalar)
+
+        square(1, 1)
+        start_roots(1)
+        unroot(1, pooled, nc.gpsimd)
+        finish_gates(1)
+        for c in range(4):
+            weigh(0, c)
+            project(3, c, (0, 1), first_bank=PACK)
+        square(2, 2)
+        square(2, 3)
+        cast(2)
+        quant_h(0, 2)
+        quant_w(2)
+        for c in range(4):
+            feature(1, c, c, (0,))
+        cast(3)
+        quant_h(2, 4)
+        quant_w(3)
+        for c in range(4):
+            feature(1, c, c, (1,))
+        cast(4)
+
+        cast_wm_pool(5)
+        square(3, 0)
+        root(2, whole)
+        square(3, 1)
+        unroot(2, whole, nc.scalar)
+        for c in range(4):
+            weigh(1, c)
+            feature(2, c, c)
+        start_roots(3)
+        quant_w(4)
+        cast_wm_rest(5)
+        quant_h(4, 8)
+        quant_w(5)
+
+        unroot(3, pooled, nc.gpsimd)
+        for view in (of_columns(POOL_COLS, 3 * HALF), of_columns(3 * HALF, WIDE)):
+            root(3, view)
+        first = [piece(0, 0, 4, g, g + 1, PACK + g) for g in range(4)]
         for part in first:
             mix(part, 0)
-        weigh(2, 0)
-        quant_wm(1)
-        weigh(2, 1)
-        weigh(2, 2)
-        quant_h(2, 0, 2)
-        mix(first[0], 1)
-        mix(first[1], 1)
-        weigh(2, 3)
-        root(3, 0, 2)
-        root(3, 2, 4)
-        store(first[0], "v")
-        quant_h(2, 2, 4)
-        mix(first[2], 1)
-        mix(first[3], 1)
+        for part in first:
+            mix(part, 1)
+        unroot(3, rest, nc.scalar)
         for c in range(4):
-            unroot(3, c, c + 1, "s")
-        last = [piece(1, 3, 4, 0, 2, 0)]
-        mix(last[0], 0)
-        store(first[2], "s")
-        store(first[3], "s")
+            weigh(2, c)
+            feature(3, c, c)
+        for part in first:
+            store(part, nc.scalar)
+        quant_h(8, 12)
         weigh(3, 0)
         weigh(3, 1)
         second = [piece(1, 0, 2, 2 * j, 2 * j + 2, PACK + j) for j in range(2)]
         for part in second:
             mix(part, 0)
-        store(first[1], "v")
-        quant_h(3, 0, 2)
+        weigh(3, 2)
+        quant_h(12, 14)
         for part in second:
             mix(part, 1)
-        last.append(piece(1, 3, 4, 2, 4, 1))
-        mix(last[1], 0)
-        weigh(3, 2)
         third = piece(1, 2, 3, 0, 4, 6)
-        mix(third, 0)
+        last = [piece(1, 3, 4, 0, 2, 7), piece(1, 3, 4, 2, 4, 0)]
+        for part in [third] + last:
+            mix(part, 0)
         weigh(3, 3)
-        quant_h(3, 2, 3)
+        quant_h(14, 15)
         mix(third, 1)
-        quant_h(3, 3, 4)
+        quant_h(15, 16)
         for part in last:
             mix(part, 1)
-        store(second[0], "s")
-        store(second[1], "s")
-        store(third, "v")
-        store(last[0], "s")
-        store(last[1], "v")
+        for part in second:
+            store(part, nc.scalar)
+        store(third, nc.vector)
+        store(last[0], nc.scalar)
+        store(last[1], nc.vector)

@@ -45,9 +45,9 @@ def tile_list_ball_cauchy_mix_kernel(tc, tab_words, tab_scales, offs, wk_words, 
 
         at_table = [0, 16 * KB]
         at_picked = [32 * KB - EDGE, 32 * KB]
-        at_rows = [35 * KB, 12 * KB]
-        at_wk_late = at_rows[0] + EDGE - 2 * KB
-        at_raw_first = at_rows[0] + HALF + H - EDGE
+        at_late_planes = 12 * KB
+        at_wk_late = 33 * KB
+        at_raw_first = 35 * KB
         at_raw = [at_raw_first, 0, 16 * KB, 24 * KB, at_raw_first, 0]
         at_root0 = 45 * KB
         at_root3 = at_raw[2]
@@ -87,7 +87,10 @@ def tile_list_ball_cauchy_mix_kernel(tc, tab_words, tab_scales, offs, wk_words, 
                 in_=wk_raw[b][:].rearrange("p a (v w t) -> p a v t w", t=PACK, w=4),
             )
 
-        picked = [placed("picked%d" % h, [P, HALF // 4], I32, at_picked[h]) for h in range(2)]
+        picked = [
+            placed("picked0", [P, (at_raw_first - at_picked[0] + EDGE) // 4], I32, at_picked[0]),
+            placed("picked1", [P, HALF // 4], I32, at_picked[1]),
+        ]
         table = [placed("table%d" % a, [P, T], I32, at_table[a]) for a in range(2)]
 
         def load_table(a):
@@ -100,39 +103,30 @@ def tile_list_ball_cauchy_mix_kernel(tc, tab_words, tab_scales, offs, wk_words, 
         nc.vector.memset(tscale[64:128, :], 0)
         nc.vector.memset(kscale[32:64, :], 0)
         nc.vector.memset(kscale[64:128, :], 0)
-        widths = [(HALF + H) // 4, HALF // 4]
         planes = [
-            [keep.tile([P, widths[h]], I32, name="plane%d%d" % (h, a), align_bytes=EDGE) for a in range(2)]
-            for h in range(2)
+            [keep.tile([P, (HALF + H) // 4], I32, name="plane0%d" % a, align_bytes=EDGE) for a in range(2)],
+            [placed("plane1%d" % a, [P, HALF // 4], I32, at_late_planes + a * HALF) for a in range(2)],
         ]
 
-        def reorder_wk_scales(dst):
-            nc.vector.tensor_copy(
-                out=dst[:, HALF // 4 :].bitcast(U16).rearrange("p (b t u) -> p b t u", b=2, t=PACK),
-                in_=kscale[:].bitcast(U16).rearrange("p (b u t) -> p b t u", b=2, t=PACK),
-            )
-
         def pick_scales(h):
-            nc.vector.memset(planes[h][1][:], 0)
             nc.vector.tensor_copy(
-                picked[h][:].bitcast(U8),
+                picked[h][:, 0 : HALF // 4].bitcast(U8),
                 tscale[:].bitcast(U8).indirect(offsets[:, h * HALF // 16 : (h + 1) * HALF // 16]),
             )
-            nc.vector.tensor_copy(planes[h][0][:, 0 : HALF // 4], picked[h][:])
-            nc.gpsimd.dma_start(planes[h][1][96:100, :], planes[h][0][28:32, :])
 
-        def move_scales(h):
-            rows = placed("rows%d" % h, [P, widths[h]], I32, at_rows[h])
-            if h == 0:
-                reorder_wk_scales(rows)
-            nc.vector.tensor_copy(rows[0:32, 0 : HALF // 4], picked[h][0:32, :])
-            for row in range(4, 28, 4):
+        def move_scales(h, queues):
+            nc.vector.memset(planes[h][1][:], 0)
+            nc.vector.tensor_copy(planes[h][0][:, 0 : HALF // 4], picked[h][:, 0 : HALF // 4])
+            for row, queue in zip(range(28, 0, -4), queues):
                 a, q = divmod(row // 4, 4)
-                nc.sync.dma_start(planes[h][a][32 * q : 32 * q + 4, :], rows[row : row + 4, :])
+                queue.dma_start(planes[h][a][32 * q : 32 * q + 4, :], planes[h][0][row : row + 4, :])
 
-        reorder_wk_scales(planes[0][0])
+        nc.vector.tensor_copy(
+            out=planes[0][0][:, HALF // 4 :].bitcast(U16).rearrange("p (b t u) -> p b t u", b=2, t=PACK),
+            in_=kscale[:].bitcast(U16).rearrange("p (b u t) -> p b t u", b=2, t=PACK),
+        )
         pick_scales(0)
-        move_scales(0)
+        move_scales(0, [nc.gpsimd] + 3 * [nc.scalar, nc.sync])
         load_table(1)
         pick_scales(1)
         permute_wk(0)
@@ -209,7 +203,11 @@ def tile_list_ball_cauchy_mix_kernel(tc, tab_words, tab_scales, offs, wk_words, 
         roots = [placed("root0", [P, WIDE], F32, at_root0)]
         roots = roots + [keep.tile([P, WIDE], F32, name="root%d" % q) for q in range(1, 3)]
         roots = roots + [placed("root3", [P, WIDE], F32, at_root3)]
-        gates = [ys[q] if q % 2 == 0 else placed("gate%d" % q, [P, WIDE], F32, at_gate[q]) for q in range(4)]
+        pool_gates = {q: placed("gate%d" % q, [P, WIDE], F32, at_gate[q]) for q in (1, 3)}
+
+        def gate(q, c):
+            return pool_gates[q] if q == 1 or (q == 3 and c >= 2) else ys[q]
+
         xs = {}
         fs = {}
 
@@ -228,30 +226,34 @@ def tile_list_ball_cauchy_mix_kernel(tc, tab_words, tab_scales, offs, wk_words, 
                     stop=(a == 1),
                 )
 
-        def chunks(tile, c0, c1):
-            return tile[:].rearrange("p (t j) -> p t j", t=PACK)[:, :, c0 * CHUNK : c1 * CHUNK]
+        def chunks(q, tile, c0, c1):
+            if q == 1:
+                return tile[:].rearrange("p (t j) -> p t j", t=PACK)[:, :, c0 * CHUNK : c1 * CHUNK]
+            pair = tile[:].rearrange("p (g t j) -> p g t j", g=2, t=PACK)[:, c0 // 2]
+            return pair[:, :, (c0 % 2) * CHUNK : (c0 % 2 + c1 - c0) * CHUNK]
 
         def square(q, t, c0=0, c1=4):
-            nc.scalar.activation(
-                out=chunks(ys[q], c0, c1)[:, t, :],
-                in_=xs[q, t, c0][:],
-                func=ACT.Square,
-                bias=bias[:, q % 2, 2 * t : 2 * t + 1],
-            )
+            src = xs[q, t, c0][:]
+            if q == 1 or c1 - c0 == 2:
+                dst = chunks(q, ys[q], c0, c1)[:, t, :]
+            else:
+                dst = ys[q][:].rearrange("p (g t j) -> p g t j", g=2, t=PACK)[:, :, t, :]
+                src = src.rearrange("p (g j) -> p g j", g=2)
+            nc.scalar.activation(out=dst, in_=src, func=ACT.Square, bias=bias[:, q % 2, 2 * t : 2 * t + 1])
             if q <= 1 and c1 == 4:
                 project(q + 1, t, (0, 1))
 
         def root(q, view):
             nc.scalar.activation(out=view(roots[q]), in_=view(ys[q]), func=ACT.Abs_reciprocal_sqrt, bias=1.0)
 
-        def unroot(q, view, eng):
+        def unroot(q, view, eng, c=0):
             if eng is nc.scalar:
-                nc.scalar.activation(out=view(gates[q]), in_=view(roots[q]), func=ACT.Square)
+                nc.scalar.activation(out=view(gate(q, c)), in_=view(roots[q]), func=ACT.Square)
             else:
-                eng.tensor_tensor(out=view(gates[q]), in0=view(roots[q]), in1=view(roots[q]), op=MULT)
+                eng.tensor_tensor(out=view(gate(q, c)), in0=view(roots[q]), in1=view(roots[q]), op=MULT)
 
-        def of_chunks(c0, c1):
-            return lambda tile: chunks(tile, c0, c1)
+        def of_chunk(c):
+            return lambda tile: chunks(0, tile, c, c + 1)
 
         def of_columns(lo, hi):
             return lambda tile: tile[:, lo:hi]
@@ -273,6 +275,14 @@ def tile_list_ball_cauchy_mix_kernel(tc, tab_words, tab_scales, offs, wk_words, 
                         stop=(a == 1 and t == PACK - 1),
                     )
 
+        slot_of = {}
+        for c in range(4):
+            slot_of[0, c] = c
+            slot_of[1, c] = 4 + c
+        for b in range(2):
+            for c in range(2):
+                slot_of[2 + b, c] = 8 + 2 * b + c
+                slot_of[2 + b, 2 + c] = 12 + 2 * c + b
         hb = {}
         hcodes = [
             placed("hcodes2", [P, HALF], U32, at_root3) if q == 2 else keep.tile([P, HALF], U32, name="hcodes%d" % q, align_bytes=EDGE)
@@ -291,11 +301,11 @@ def tile_list_ball_cauchy_mix_kernel(tc, tab_words, tab_scales, offs, wk_words, 
             return hb[g][:, (s0 - 4 * g) * PASS : (s1 - 4 * g) * PASS]
 
         def weigh(q, c):
-            s0 = 4 * q + c
+            s0 = slot_of[q, c]
             nc.vector.tensor_tensor(
                 out=h_slots(s0, s0 + 1).rearrange("p (u i t) -> p u t i", i=2, t=PACK),
                 in0=fs[q, c][:].rearrange("p t (u i) -> p u t i", i=2),
-                in1=chunks(gates[q], c, c + 1).rearrange("p t (u i) -> p u t i", i=2),
+                in1=chunks(q, gate(q, c), c, c + 1).rearrange("p t (u i) -> p u t i", i=2),
                 op=MULT,
             )
 
@@ -314,7 +324,7 @@ def tile_list_ball_cauchy_mix_kernel(tc, tab_words, tab_scales, offs, wk_words, 
         def mix(part, b):
             acc, h, c0, c1, g0, g1 = part
             codes, scales = quantised[4 + b]
-            s0 = 4 * (2 * h + b) + c0
+            s0 = slot_of[2 * h + b, c0]
             cols = slice(s0 * CHUNK, (s0 + c1 - c0) * CHUNK)
             for g in range(g0, g1):
                 nc.tensor.matmul_mx(
@@ -341,7 +351,7 @@ def tile_list_ball_cauchy_mix_kernel(tc, tab_words, tab_scales, offs, wk_words, 
         load_wk(1)
         load_wf(0)
         load_wf(1)
-        move_scales(1)
+        move_scales(1, [nc.gpsimd] + 6 * [nc.sync])
         load_wf(2)
         load_wf(3)
         gather(1, 0, HALF // 2)
@@ -359,11 +369,13 @@ def tile_list_ball_cauchy_mix_kernel(tc, tab_words, tab_scales, offs, wk_words, 
         for t in range(PACK):
             project(0, t, (1,), 2, 4, 0)
 
+        front = of_columns(0, WIDE // 2)
+        back = of_columns(WIDE // 2, WIDE)
         cast(0)
         load_wm(0)
         square(0, 0, 2, 4)
-        root(0, of_chunks(0, 2))
-        unroot(0, of_chunks(0, 2), nc.vector)
+        root(0, front)
+        unroot(0, front, nc.vector)
         quant_w(0)
         for c in range(4):
             feature(0, c, PACK + c, (0,))
@@ -372,16 +384,15 @@ def tile_list_ball_cauchy_mix_kernel(tc, tab_words, tab_scales, offs, wk_words, 
         cast(1)
         load_wm(1)
         square(1, 0)
-        root(0, of_chunks(2, 4))
-        unroot(0, of_chunks(2, 3), nc.vector)
+        root(0, back)
+        unroot(0, of_chunk(2), nc.vector)
         quant_w(1)
         for c in range(4):
             feature(0, c, PACK + c, (1,))
-        unroot(0, of_chunks(3, 4), nc.vector)
+        unroot(0, of_chunk(3), nc.vector)
 
         pooled = of_columns(0, POOL_COLS)
         rest = of_columns(POOL_COLS, WIDE)
-        whole = of_columns(0, WIDE)
 
         def start_roots(q):
             square(q, 2)
@@ -416,55 +427,59 @@ def tile_list_ball_cauchy_mix_kernel(tc, tab_words, tab_scales, offs, wk_words, 
         cast(4)
 
         cast_wm_pool(5)
-        square(3, 0)
-        root(2, whole)
-        square(3, 1)
-        unroot(2, whole, nc.scalar)
+        for t in range(PACK):
+            square(3, t)
+        root(2, front)
+        root(3, front)
+        root(3, back)
+        unroot(2, front, nc.scalar)
+        unroot(3, front, nc.scalar)
+        root(2, back)
+        early = [(2, 0), (2, 1), (3, 0), (3, 1)]
+        late = [(2, 2), (3, 2), (2, 3), (3, 3)]
         for c in range(4):
             weigh(1, c)
-            feature(2, c, c)
-        start_roots(3)
+            feature(early[c][0], early[c][1], c)
         quant_w(4)
         cast_wm_rest(5)
         quant_h(4, 8)
         quant_w(5)
 
-        unroot(3, pooled, nc.gpsimd)
-        for view in (of_columns(POOL_COLS, 3 * HALF), of_columns(3 * HALF, WIDE)):
-            root(3, view)
+        unroot(3, back, nc.gpsimd, 2)
         first = [piece(0, 0, 4, g, g + 1, PACK + g) for g in range(4)]
         for part in first:
             mix(part, 0)
         for part in first:
             mix(part, 1)
-        unroot(3, rest, nc.scalar)
-        for c in range(4):
-            weigh(2, c)
-            feature(3, c, c)
-        for part in first:
+        store(first[0], nc.scalar)
+        unroot(2, back, nc.scalar)
+        for i in range(4):
+            weigh(early[i][0], early[i][1])
+            feature(late[i][0], late[i][1], i)
+        for part in first[1:]:
             store(part, nc.scalar)
+        weigh(2, 2)
         quant_h(8, 12)
-        weigh(3, 0)
-        weigh(3, 1)
         second = [piece(1, 0, 2, 2 * j, 2 * j + 2, PACK + j) for j in range(2)]
         for part in second:
             mix(part, 0)
-        weigh(3, 2)
-        quant_h(12, 14)
-        for part in second:
             mix(part, 1)
+        weigh(3, 2)
+        weigh(2, 3)
+        quant_h(12, 14)
         third = piece(1, 2, 3, 0, 4, 6)
+        mix(third, 0)
+        mix(third, 1)
+        quant_h(14, 15)
         last = [piece(1, 3, 4, 0, 2, 7), piece(1, 3, 4, 2, 4, 0)]
-        for part in [third] + last:
+        for part in last:
             mix(part, 0)
         weigh(3, 3)
-        quant_h(14, 15)
-        mix(third, 1)
         quant_h(15, 16)
         for part in last:
             mix(part, 1)
         for part in second:
             store(part, nc.scalar)
-        store(third, nc.vector)
+        store(third, nc.scalar)
         store(last[0], nc.scalar)
         store(last[1], nc.vector)

@@ -172,8 +172,8 @@ def tile_list_ball_cauchy_mix_kernel(tc, tab_words, tab_scales, offs, wk_words, 
                 )
             else:
                 nc.vector.tensor_copy(
-                    out=rounded[i][:].rearrange("p (c i j) -> p c j i", i=2, j=PACK),
-                    in_=raws[i][:].rearrange("p j (c i) -> p c j i", i=2),
+                    out=rounded[i][:].rearrange("p (c i j) -> p c j i", i=4, j=PACK),
+                    in_=raws[i][:].rearrange("p j (c i) -> p c j i", i=4),
                 )
 
         def cast_wm_pool(i):
@@ -189,8 +189,8 @@ def tile_list_ball_cauchy_mix_kernel(tc, tab_words, tab_scales, offs, wk_words, 
 
         def cast_wm_rest(i):
             nc.vector.tensor_copy(
-                out=rounded[i][:, POOL_CAST * PACK :].rearrange("p (c i j) -> p c j i", i=2, j=PACK),
-                in_=raws[i][:, :, POOL_CAST:].rearrange("p j (c i) -> p c j i", i=2),
+                out=rounded[i][:, POOL_CAST * PACK :].rearrange("p (c i j) -> p c j i", i=4, j=PACK),
+                in_=raws[i][:, :, POOL_CAST:].rearrange("p j (c i) -> p c j i", i=4),
             )
 
         def quant_w(i):
@@ -346,8 +346,7 @@ def tile_list_ball_cauchy_mix_kernel(tc, tab_words, tab_scales, offs, wk_words, 
                 nc.scalar.copy(out=res[:], in_=acc[:])
             nc.sync.dma_start(out_view[:, g0:g1, h * HALF + c0 * CHUNK : h * HALF + c1 * CHUNK], res[:])
 
-        gather(0, 0, HALF)
-        gather(0, HALF, S)
+        gather(0, 0, S)
         load_wk(1)
         load_wf(0)
         load_wf(1)

@@ -159,9 +159,9 @@ def tile_list_ball_cauchy_mix_kernel(tc, tab_words, tab_scales, offs, wk_words, 
             nc.sync.dma_start(raws[i][:], src.rearrange("(p j) c -> p j c", j=PACK))
 
         def load_wm(b):
-            src = wm[b * PASS : (b + 1) * PASS, :].rearrange("(u t e) c -> e u t c", t=PACK, e=2)
-            for e in range(2):
-                nc.sync.dma_start(raws[4 + b][e:P:2], src[e])
+            src = wm[b * PASS : (b + 1) * PASS, :].rearrange("(u t e) c -> t u e c", t=PACK, e=2)
+            for t in range(PACK):
+                nc.sync.dma_start(raws[4 + b][:, t, :], src[t])
 
         def cast(i):
             rounded[i] = placed("rounded%d" % i, [P, WIDE], BF16, at_rounded[i])

@@ -67,9 +67,9 @@ def tile_list_ball_cauchy_mix_kernel(tc, tab_words, tab_scales, offs, wk_words, 
         nc.gpsimd.memset(warm[:, 0:1], 1.0)
         nc.scalar.activation(out=warm[:, 1:2], in_=warm[:, 0:1], func=ACT.Abs_reciprocal_sqrt)
 
-        bias = keep.tile([P, 2, 8], F32, name="bias", align_bytes=EDGE)
-        for e in range(2):
-            nc.gpsimd.dma_start(bias[e:P:2, :, 0:7], bk.rearrange("(b u k) -> u b k", b=2, k=8)[:, :, e : e + 7])
+        bias = keep.tile([P, 2, 16], F32, name="bias", align_bytes=EDGE)
+        for e in range(PACK):
+            nc.gpsimd.dma_start(bias[e:P:PACK, :, 0:13], bk.rearrange("(b u k) -> u b k", b=2, k=16)[:, :, e : e + 13])
 
         wk_view = wk_words.rearrange("a p c -> p a c")
         wk_raw = [
@@ -83,8 +83,8 @@ def tile_list_ball_cauchy_mix_kernel(tc, tab_words, tab_scales, offs, wk_words, 
 
         def permute_wk(b):
             nc.vector.tensor_copy(
-                out=wkp[b][:].rearrange("p a (t v w) -> p a v t w", t=PACK, w=4),
-                in_=wk_raw[b][:].rearrange("p a (v w t) -> p a v t w", t=PACK, w=4),
+                out=wkp[b][:].rearrange("p a (t u w) -> p a t u w", t=PACK, w=2),
+                in_=wk_raw[b][:].rearrange("p a (u t w) -> p a t u w", t=PACK, w=2),
             )
 
         picked = [
@@ -122,8 +122,8 @@ def tile_list_ball_cauchy_mix_kernel(tc, tab_words, tab_scales, offs, wk_words, 
                 queue.dma_start(planes[h][a][32 * q : 32 * q + 4, :], planes[h][0][row : row + 4, :])
 
         nc.vector.tensor_copy(
-            out=planes[0][0][:, HALF // 4 :].bitcast(U16).rearrange("p (b t u) -> p b t u", b=2, t=PACK),
-            in_=kscale[:].bitcast(U16).rearrange("p (b u t) -> p b t u", b=2, t=PACK),
+            out=planes[0][0][:, HALF // 4 :].rearrange("p (b t u) -> p b t u", b=2, t=PACK),
+            in_=kscale[:].rearrange("p (b u t) -> p b t u", b=2, t=PACK),
         )
         pick_scales(0)
         move_scales(0, [nc.gpsimd] + 3 * [nc.scalar, nc.sync])
@@ -159,7 +159,7 @@ def tile_list_ball_cauchy_mix_kernel(tc, tab_words, tab_scales, offs, wk_words, 
             nc.sync.dma_start(raws[i][:], src.rearrange("(p j) c -> p j c", j=PACK))
 
         def load_wm(b):
-            src = wm[b * PASS : (b + 1) * PASS, :].rearrange("(u t e) c -> t u e c", t=PACK, e=2)
+            src = wm[b * PASS : (b + 1) * PASS, :].rearrange("(u t e) c -> t u e c", t=PACK, e=PACK)
             for t in range(PACK):
                 nc.sync.dma_start(raws[4 + b][:, t, :], src[t])
 
@@ -167,8 +167,8 @@ def tile_list_ball_cauchy_mix_kernel(tc, tab_words, tab_scales, offs, wk_words, 
             rounded[i] = placed("rounded%d" % i, [P, WIDE], BF16, at_rounded[i])
             if i < 4:
                 nc.vector.tensor_copy(
-                    out=rounded[i][:].rearrange("p (t u e j) -> p t u j e", t=PACK, e=2, j=PACK),
-                    in_=raws[i][:].rearrange("p j (u t e) -> p t u j e", t=PACK, e=2),
+                    out=rounded[i][:].rearrange("p (t u e j) -> p t u j e", t=PACK, e=PACK, j=PACK),
+                    in_=raws[i][:].rearrange("p j (u t e) -> p t u j e", t=PACK, e=PACK),
                 )
             else:
                 nc.vector.tensor_copy(
@@ -239,7 +239,7 @@ def tile_list_ball_cauchy_mix_kernel(tc, tab_words, tab_scales, offs, wk_words, 
             else:
                 dst = ys[q][:].rearrange("p (g t j) -> p g t j", g=2, t=PACK)[:, :, t, :]
                 src = src.rearrange("p (g j) -> p g j", g=2)
-            nc.scalar.activation(out=dst, in_=src, func=ACT.Square, bias=bias[:, q % 2, 2 * t : 2 * t + 1])
+            nc.scalar.activation(out=dst, in_=src, func=ACT.Square, bias=bias[:, q % 2, PACK * t : PACK * t + 1])
             if q <= 1 and c1 == 4:
                 project(q + 1, t, (0, 1))
 

@@ -117,7 +117,7 @@ def tile_list_ball_cauchy_mix_kernel(tc, tab_words, tab_scales, offs, wk_words, 
         def move_scales(h, queues):
             nc.vector.memset(planes[h][1][:], 0)
             nc.vector.tensor_copy(planes[h][0][:, 0 : HALF // 4], picked[h][:, 0 : HALF // 4])
-            for row, queue in zip(range(28, 0, -4), queues):
+            for row, queue in queues:
                 a, q = divmod(row // 4, 4)
                 queue.dma_start(planes[h][a][32 * q : 32 * q + 4, :], planes[h][0][row : row + 4, :])
 
@@ -126,7 +126,7 @@ def tile_list_ball_cauchy_mix_kernel(tc, tab_words, tab_scales, offs, wk_words, 
             in_=kscale[:].rearrange("p (b u t) -> p b t u", b=2, t=PACK),
         )
         pick_scales(0)
-        move_scales(0, [nc.gpsimd] + 3 * [nc.scalar, nc.sync])
+        move_scales(0, [(28, nc.gpsimd), (4, nc.sync), (8, nc.scalar), (12, nc.sync), (16, nc.scalar), (20, nc.scalar), (24, nc.scalar)])
         load_table(1)
         pick_scales(1)
         permute_wk(0)
@@ -303,9 +303,9 @@ def tile_list_ball_cauchy_mix_kernel(tc, tab_words, tab_scales, offs, wk_words, 
         def weigh(q, c):
             s0 = slot_of[q, c]
             nc.vector.tensor_tensor(
-                out=h_slots(s0, s0 + 1).rearrange("p (u i t) -> p u t i", i=2, t=PACK),
-                in0=fs[q, c][:].rearrange("p t (u i) -> p u t i", i=2),
-                in1=chunks(q, gate(q, c), c, c + 1).rearrange("p t (u i) -> p u t i", i=2),
+                out=h_slots(s0, s0 + 1).rearrange("p (u i t) -> p u t i", i=4, t=PACK),
+                in0=fs[q, c][:].rearrange("p t (u i) -> p u t i", i=4),
+                in1=chunks(q, gate(q, c), c, c + 1).rearrange("p t (u i) -> p u t i", i=4),
                 op=MULT,
             )
 
@@ -350,7 +350,7 @@ def tile_list_ball_cauchy_mix_kernel(tc, tab_words, tab_scales, offs, wk_words, 
         load_wk(1)
         load_wf(0)
         load_wf(1)
-        move_scales(1, [nc.gpsimd] + 6 * [nc.sync])
+        move_scales(1, [(28, nc.gpsimd)] + [(row, nc.sync) for row in range(24, 0, -4)])
         load_wf(2)
         load_wf(3)
         gather(1, 0, HALF // 2)

@@ -25,8 +25,8 @@ CHUNK = 128
 WIDE = PACK * HALF
 KB = 1024
 EDGE = 64
-POOL_COLS = 896
-POOL_CAST = 320
+POOL_COLS = 640
+POOL_CAST = 384
 
 
 def tile_list_ball_cauchy_mix_kernel(tc, tab_words, tab_scales, offs, wk_words, wk_scales, bk, wf, wm, out):
@@ -49,9 +49,9 @@ def tile_list_ball_cauchy_mix_kernel(tc, tab_words, tab_scales, offs, wk_words, 
         at_wk_late = 33 * KB
         at_raw_first = 35 * KB
         at_raw = [at_raw_first, 0, 16 * KB, 24 * KB, at_raw_first, 0]
-        at_root0 = 45 * KB
+        at_root0 = 48 * KB
         at_root3 = at_raw[2]
-        at_rounded = [57 * KB, at_root0 + 8 * KB, 61 * KB, 57 * KB, 61 * KB, at_raw[4]]
+        at_rounded = [60 * KB, at_root0 + 8 * KB, at_root0 + EDGE - 4 * KB, 60 * KB, at_root0 + EDGE - 4 * KB, at_raw[4]]
         at_gate = [None, at_rounded[1] + EDGE - 8 * KB, None, at_rounded[5] + EDGE - 8 * KB]
         at_h = [8 * KB, at_raw[4] + 4 * KB, at_rounded[5] + EDGE]
 
@@ -176,6 +176,23 @@ def tile_list_ball_cauchy_mix_kernel(tc, tab_words, tab_scales, offs, wk_words, 
                     in_=raws[i][:].rearrange("p j (c i) -> p c j i", i=4),
                 )
 
+        def cast_wf_pool(i):
+            rounded[i] = placed("rounded%d" % i, [P, WIDE], BF16, at_rounded[i])
+            nc.gpsimd.tensor_scalar(
+                out=rounded[i][:, 0:PASS].rearrange("p (u e j) -> p u j e", e=PACK, j=PACK),
+                in0=raws[i][:].rearrange("p j (u t e) -> p t u j e", t=PACK, e=PACK)[:, 0],
+                scalar1=1.0,
+                scalar2=0.0,
+                op0=MULT,
+                op1=ADD,
+            )
+
+        def cast_wf_rest(i):
+            nc.vector.tensor_copy(
+                out=rounded[i][:].rearrange("p (t u e j) -> p u t j e", t=PACK, e=PACK, j=PACK)[:, :, 1:],
+                in_=raws[i][:].rearrange("p j (u t e) -> p u t j e", t=PACK, e=PACK)[:, :, 1:],
+            )
+
         def cast_wm_pool(i):
             rounded[i] = placed("rounded%d" % i, [P, WIDE], BF16, at_rounded[i])
             nc.gpsimd.tensor_scalar(
@@ -205,7 +222,11 @@ def tile_list_ball_cauchy_mix_kernel(tc, tab_words, tab_scales, offs, wk_words, 
         roots = roots + [placed("root3", [P, WIDE], F32, at_root3)]
         pool_gates = {q: placed("gate%d" % q, [P, WIDE], F32, at_gate[q]) for q in (1, 3)}
 
+        third_gates = [placed("gate2%d" % g, [P, WIDE], F32, 64 * KB + g * (8 * KB - EDGE)) for g in range(2)]
+
         def gate(q, c):
+            if q == 2:
+                return third_gates[c // 2]
             return pool_gates[q] if q == 1 or (q == 3 and c >= 2) else ys[q]
 
         xs = {}
@@ -321,7 +342,7 @@ def tile_list_ball_cauchy_mix_kernel(tc, tab_words, tab_scales, offs, wk_words, 
         def piece(h, c0, c1, g0, g1, i):
             return bank(i, [P, g1 - g0, (c1 - c0) * CHUNK]), h, c0, c1, g0, g1
 
-        def mix(part, b):
+        def mix(part, b, opening=0):
             acc, h, c0, c1, g0, g1 = part
             codes, scales = quantised[4 + b]
             s0 = slot_of[2 * h + b, c0]
@@ -333,18 +354,18 @@ def tile_list_ball_cauchy_mix_kernel(tc, tab_words, tab_scales, offs, wk_words, 
                     lhsT_scale=scales[:, g * P : (g + 1) * P],
                     rhs=h_codes(s0, s0 + c1 - c0),
                     rhs_scale=hscales[:, cols],
-                    start=(b == 0 and g == g0),
-                    stop=(b == 1 and g == g1 - 1),
+                    start=(b == opening and g == g0),
+                    stop=(b != opening and g == g1 - 1),
                 )
 
-        def store(part, eng):
+        def store(part, eng, queue=nc.sync):
             acc, h, c0, c1, g0, g1 = part
             res = opool.tile(list(acc.shape), F32, name="res", tag="res")
             if eng is nc.vector:
                 nc.vector.tensor_copy(out=res[:], in_=acc[:])
             else:
                 nc.scalar.copy(out=res[:], in_=acc[:])
-            nc.sync.dma_start(out_view[:, g0:g1, h * HALF + c0 * CHUNK : h * HALF + c1 * CHUNK], res[:])
+            queue.dma_start(out_view[:, g0:g1, h * HALF + c0 * CHUNK : h * HALF + c1 * CHUNK], res[:])
 
         gather(0, 0, S)
         load_wk(1)
@@ -404,6 +425,7 @@ def tile_list_ball_cauchy_mix_kernel(tc, tab_words, tab_scales, offs, wk_words, 
             square(q + 1, 1)
             unroot(q, rest, nc.scalar)
 
+        cast_wf_pool(2)
         square(1, 1)
         start_roots(1)
         unroot(1, pooled, nc.gpsimd)
@@ -413,7 +435,7 @@ def tile_list_ball_cauchy_mix_kernel(tc, tab_words, tab_scales, offs, wk_words, 
             project(3, c, (0, 1), first_bank=PACK)
         square(2, 2)
         square(2, 3)
-        cast(2)
+        cast_wf_rest(2)
         quant_h(0, 2)
         quant_w(2)
         for c in range(4):
@@ -435,7 +457,7 @@ def tile_list_ball_cauchy_mix_kernel(tc, tab_words, tab_scales, offs, wk_words, 
         unroot(3, front, nc.scalar)
         root(2, back)
         early = [(2, 0), (2, 1), (3, 0), (3, 1)]
-        late = [(2, 2), (3, 2), (2, 3), (3, 3)]
+        late = [(3, 2), (2, 2), (3, 3), (2, 3)]
         for c in range(4):
             weigh(1, c)
             feature(early[c][0], early[c][1], c)
@@ -444,41 +466,42 @@ def tile_list_ball_cauchy_mix_kernel(tc, tab_words, tab_scales, offs, wk_words, 
         quant_h(4, 8)
         quant_w(5)
 
-        unroot(3, back, nc.gpsimd, 2)
+        for c in (2, 3):
+            unroot(3, of_chunk(c), nc.gpsimd, 2)
         first = [piece(0, 0, 4, g, g + 1, PACK + g) for g in range(4)]
         for part in first:
             mix(part, 0)
         for part in first:
             mix(part, 1)
-        store(first[0], nc.scalar)
-        unroot(2, back, nc.scalar)
         for i in range(4):
             weigh(early[i][0], early[i][1])
             feature(late[i][0], late[i][1], i)
-        for part in first[1:]:
-            store(part, nc.scalar)
-        weigh(2, 2)
+        for c in (2, 3):
+            for part in first[2 * c - 4 : 2 * c - 2]:
+                store(part, nc.scalar)
+            unroot(2, of_chunk(c), nc.scalar, c)
+        weigh(3, 2)
         quant_h(8, 12)
         second = [piece(1, 0, 2, 2 * j, 2 * j + 2, PACK + j) for j in range(2)]
         for part in second:
             mix(part, 0)
             mix(part, 1)
-        weigh(3, 2)
-        weigh(2, 3)
+        weigh(2, 2)
+        weigh(3, 3)
         quant_h(12, 14)
         third = piece(1, 2, 3, 0, 4, 6)
         mix(third, 0)
         mix(third, 1)
-        quant_h(14, 15)
+        quant_h(15, 16)
         last = [piece(1, 3, 4, 0, 2, 7), piece(1, 3, 4, 2, 4, 0)]
         for part in last:
-            mix(part, 0)
-        weigh(3, 3)
-        quant_h(15, 16)
+            mix(part, 1, 1)
+        weigh(2, 3)
+        quant_h(14, 15)
         for part in last:
-            mix(part, 1)
+            mix(part, 0, 1)
         for part in second:
             store(part, nc.scalar)
         store(third, nc.scalar)
-        store(last[0], nc.scalar)
+        store(last[0], nc.scalar, nc.scalar)
         store(last[1], nc.vector)

@@ -179,8 +179,8 @@ def tile_list_ball_cauchy_mix_kernel(tc, tab_words, tab_scales, offs, wk_words, 
         def cast_wf_pool(i):
             rounded[i] = placed("rounded%d" % i, [P, WIDE], BF16, at_rounded[i])
             nc.gpsimd.tensor_scalar(
-                out=rounded[i][:, 0:PASS].rearrange("p (u e j) -> p u j e", e=PACK, j=PACK),
-                in0=raws[i][:].rearrange("p j (u t e) -> p t u j e", t=PACK, e=PACK)[:, 0],
+                out=rounded[i][:, 0:PASS].rearrange("p (u e j) -> p u e j", e=PACK, j=PACK),
+                in0=raws[i][:].rearrange("p j (u t e) -> p t u e j", t=PACK, e=PACK)[:, 0],
                 scalar1=1.0,
                 scalar2=0.0,
                 op0=MULT,
@@ -451,8 +451,7 @@ def tile_list_ball_cauchy_mix_kernel(tc, tab_words, tab_scales, offs, wk_words, 
         for t in range(PACK):
             square(3, t)
         root(2, front)
-        root(3, front)
-        root(3, back)
+        root(3, of_columns(0, WIDE))
         unroot(2, front, nc.scalar)
         unroot(3, front, nc.scalar)
         root(2, back)
@@ -492,11 +491,11 @@ def tile_list_ball_cauchy_mix_kernel(tc, tab_words, tab_scales, offs, wk_words, 
         third = piece(1, 2, 3, 0, 4, 6)
         mix(third, 0)
         mix(third, 1)
+        weigh(2, 3)
         quant_h(15, 16)
         last = [piece(1, 3, 4, 0, 2, 7), piece(1, 3, 4, 2, 4, 0)]
         for part in last:
             mix(part, 1, 1)
-        weigh(2, 3)
         quant_h(14, 15)
         for part in last:
             mix(part, 0, 1)

@@ -25,7 +25,7 @@ CHUNK = 128
 WIDE = PACK * HALF
 KB = 1024
 EDGE = 64
-POOL_COLS = 640
+POOL_COLS = 896
 POOL_CAST = 384
 
 
@@ -175,23 +175,6 @@ def tile_list_ball_cauchy_mix_kernel(tc, tab_words, tab_scales, offs, wk_words, 
                     out=rounded[i][:].rearrange("p (c i j) -> p c j i", i=4, j=PACK),
                     in_=raws[i][:].rearrange("p j (c i) -> p c j i", i=4),
                 )
-
-        def cast_wf_pool(i):
-            rounded[i] = placed("rounded%d" % i, [P, WIDE], BF16, at_rounded[i])
-            nc.gpsimd.tensor_scalar(
-                out=rounded[i][:, 0:PASS].rearrange("p (u e j) -> p u e j", e=PACK, j=PACK),
-                in0=raws[i][:].rearrange("p j (u t e) -> p t u e j", t=PACK, e=PACK)[:, 0],
-                scalar1=1.0,
-                scalar2=0.0,
-                op0=MULT,
-                op1=ADD,
-            )
-
-        def cast_wf_rest(i):
-            nc.vector.tensor_copy(
-                out=rounded[i][:].rearrange("p (t u e j) -> p u t j e", t=PACK, e=PACK, j=PACK)[:, :, 1:],
-                in_=raws[i][:].rearrange("p j (u t e) -> p u t j e", t=PACK, e=PACK)[:, :, 1:],
-            )
 
         def cast_wm_pool(i):
             rounded[i] = placed("rounded%d" % i, [P, WIDE], BF16, at_rounded[i])
@@ -425,7 +408,6 @@ def tile_list_ball_cauchy_mix_kernel(tc, tab_words, tab_scales, offs, wk_words, 
             square(q + 1, 1)
             unroot(q, rest, nc.scalar)
 
-        cast_wf_pool(2)
         square(1, 1)
         start_roots(1)
         unroot(1, pooled, nc.gpsimd)
@@ -435,7 +417,7 @@ def tile_list_ball_cauchy_mix_kernel(tc, tab_words, tab_scales, offs, wk_words, 
             project(3, c, (0, 1), first_bank=PACK)
         square(2, 2)
         square(2, 3)
-        cast_wf_rest(2)
+        cast(2)
         quant_h(0, 2)
         quant_w(2)
         for c in range(4):

@@ -457,10 +457,11 @@ def tile_list_ball_cauchy_mix_kernel(tc, tab_words, tab_scales, offs, wk_words, 
         for i in range(4):
             weigh(early[i][0], early[i][1])
             feature(late[i][0], late[i][1], i)
-        for c in (2, 3):
-            for part in first[2 * c - 4 : 2 * c - 2]:
-                store(part, nc.scalar)
-            unroot(2, of_chunk(c), nc.scalar, c)
+        for part in first[:3]:
+            store(part, nc.scalar)
+        unroot(2, of_chunk(2), nc.scalar, 2)
+        store(first[3], nc.scalar)
+        unroot(2, of_chunk(3), nc.scalar, 3)
         weigh(3, 2)
         quant_h(8, 12)
         second = [piece(1, 0, 2, 2 * j, 2 * j + 2, PACK + j) for j in range(2)]

from contextlib import ExitStack

import concourse.mybir as mybir

K, T, S, H, N = 1024, 4096, 1024, 1024, 512
FLOPS = 2 * S * (K * H + K * H + H * N)

F32 = mybir.dt.float32
BF16 = mybir.dt.bfloat16
I32 = mybir.dt.int32
U32 = mybir.dt.uint32
U16 = mybir.dt.uint16
U8 = mybir.dt.uint8
FP8X4 = mybir.dt.float8_e4m3fn_x4
FP4X4 = mybir.dt.float4_e2m1fn_x4
ACT = mybir.ActivationFunctionType
MULT = mybir.AluOpType.mult
ADD = mybir.AluOpType.add

P = 128
PACK = 4
PASS = P * PACK
HALF = 512
CHUNK = 128
WIDE = PACK * HALF
KB = 1024
EDGE = 64
POOL_COLS = 896
POOL_CAST = 384


def tile_list_ball_cauchy_mix_kernel(tc, tab_words, tab_scales, offs, wk_words, wk_scales, bk, wf, wm, out):
    nc = tc.nc
    with ExitStack() as ctx:
        keep = ctx.enter_context(tc.tile_pool(name="keep", bufs=1))
        stage = ctx.enter_context(tc.tile_pool(name="stage", bufs=1))
        opool = ctx.enter_context(tc.tile_pool(name="opool", bufs=9))
        psum = ctx.enter_context(tc.psum_pool(name="psum", bufs=1))

        def bank(i, shape):
            return psum.tile(shape, F32, name="bank%d" % i, tag="bank%d" % i)

        def placed(name, shape, dtype, at):
            return stage.tile(shape, dtype, name=name, align_bytes=EDGE, offset=at)

        at_table = [0, 16 * KB]
        at_picked = [32 * KB - EDGE, 32 * KB]
        at_late_planes = 12 * KB
        at_wk_late = 33 * KB
        at_raw_first = 35 * KB
        at_raw = [at_raw_first, 0, 16 * KB, 24 * KB, at_raw_first, 0]
        at_root0 = 48 * KB
        at_root3 = at_raw[2]
        at_rounded = [60 * KB, at_root0 + 8 * KB, at_root0 + EDGE - 4 * KB, 60 * KB, at_root0 + EDGE - 4 * KB, at_raw[4]]
        at_gate = [None, at_rounded[1] + EDGE - 8 * KB, None, at_rounded[5] + EDGE - 8 * KB]
        at_h = [8 * KB, at_raw[4] + 4 * KB, at_rounded[5] + EDGE]

        offsets = keep.tile([P, S // 16], U16, name="offsets")
        nc.sync.dma_start(offsets[:], offs)

        tscale = keep.tile([P, T // 4], I32, name="tscale", align_bytes=EDGE)
        nc.sync.dma_start(tscale[0:32, :], tab_scales.rearrange("a q c -> (a q) c").bitcast(I32))
        kscale = keep.tile([P, H // 4], I32, name="kscale", align_bytes=EDGE)
        nc.sync.dma_start(kscale[0:32, :], wk_scales.rearrange("a q c -> (a q) c").bitcast(I32))

        warm = keep.tile([P, 2], F32, name="warm")
        nc.gpsimd.memset(warm[:, 0:1], 1.0)
        nc.scalar.activation(out=warm[:, 1:2], in_=warm[:, 0:1], func=ACT.Abs_reciprocal_sqrt)

        bias = keep.tile([P, 2, 16], F32, name="bias", align_bytes=EDGE)
        for e in range(PACK):
            nc.gpsimd.dma_start(bias[e:P:PACK, :, 0:13], bk.rearrange("(b u k) -> u b k", b=2, k=16)[:, :, e : e + 13])

        wk_view = wk_words.rearrange("a p c -> p a c")
        wk_raw = [
            keep.tile([P, 2, PASS // 2], I32, name="wk_raw0", align_bytes=EDGE),
            placed("wk_raw1", [P, 2, PASS // 2], I32, at_wk_late),
        ]
        wkp = [keep.tile([P, 2, PASS // 2], I32, name="wkp%d" % b, align_bytes=EDGE) for b in range(2)]

        def load_wk(b):
            nc.sync.dma_start(wk_raw[b][:], wk_view[:, :, 2 * PASS * b : 2 * PASS * (b + 1)].bitcast(I32))

        def permute_wk(b):
            nc.vector.tensor_copy(
                out=wkp[b][:].rearrange("p a (t u w) -> p a t u w", t=PACK, w=2),
                in_=wk_raw[b][:].rearrange("p a (u t w) -> p a t u w", t=PACK, w=2),
            )

        picked = [
            placed("picked0", [P, (at_raw_first - at_picked[0] + EDGE) // 4], I32, at_picked[0]),
            placed("picked1", [P, HALF // 4], I32, at_picked[1]),
        ]
        table = [placed("table%d" % a, [P, T], I32, at_table[a]) for a in range(2)]

        def load_table(a):
            nc.sync.dma_start(table[a][:], tab_words[a].rearrange("p n t -> p (n t)").bitcast(I32))

        load_wk(0)
        load_table(0)

        nc.vector.memset(tscale[32:64, :], 0)
        nc.vector.memset(tscale[64:128, :], 0)
        nc.vector.memset(kscale[32:64, :], 0)
        nc.vector.memset(kscale[64:128, :], 0)
        planes = [
            [keep.tile([P, (HALF + H) // 4], I32, name="plane0%d" % a, align_bytes=EDGE) for a in range(2)],
            [placed("plane1%d" % a, [P, HALF // 4], I32, at_late_planes + a * HALF) for a in range(2)],
        ]

        def pick_scales(h):
            nc.vector.tensor_copy(
                picked[h][:, 0 : HALF // 4].bitcast(U8),
                tscale[:].bitcast(U8).indirect(offsets[:, h * HALF // 16 : (h + 1) * HALF // 16]),
            )

        def move_scales(h, queues):
            nc.vector.memset(planes[h][1][:], 0)
            nc.vector.tensor_copy(planes[h][0][:, 0 : HALF // 4], picked[h][:, 0 : HALF // 4])
            for row, queue in queues:
                a, q = divmod(row // 4, 4)
                queue.dma_start(planes[h][a][32 * q : 32 * q + 4, :], planes[h][0][row : row + 4, :])

        nc.vector.tensor_copy(
            out=planes[0][0][:, HALF // 4 :].rearrange("p (b t u) -> p b t u", b=2, t=PACK),
            in_=kscale[:].rearrange("p (b u t) -> p b t u", b=2, t=PACK),
        )
        pick_scales(0)
        move_scales(0, [(28, nc.gpsimd), (4, nc.sync), (8, nc.scalar), (12, nc.sync), (16, nc.scalar), (20, nc.scalar), (24, nc.scalar)])
        load_table(1)
        pick_scales(1)
        permute_wk(0)

        def token_scales(a, h, c0, c1):
            return planes[h][a][:].bitcast(U8)[:, c0 * CHUNK : c1 * CHUNK]

        def wk_scale(a, b, t):
            k0 = HALF + b * PASS + t * P
            return planes[0][a][:].bitcast(U8)[:, k0 : k0 + P]

        vw = [keep.tile([P, S], I32, name="vw%d" % a, align_bytes=EDGE) for a in range(2)]

        def gather(a, j0, j1):
            nc.vector.tensor_copy(
                vw[a][:, j0:j1].bitcast(U32),
                table[a][:].bitcast(U32).indirect(offsets[:, j0 // 16 : j1 // 16]),
            )

        def tokens(a, h, c0, c1):
            return vw[a][:, h * HALF + c0 * CHUNK : h * HALF + c1 * CHUNK].bitcast(FP8X4)

        raws = [placed("raw%d" % i, [P, PACK, HALF], F32, at_raw[i]) for i in range(6)]
        rounded = {}
        quantised = {}

        def load_wf(i):
            b, a = divmod(i, 2)
            src = wf[a * PASS : (a + 1) * PASS, b * PASS : (b + 1) * PASS]
            nc.sync.dma_start(raws[i][:], src.rearrange("(p j) c -> p j c", j=PACK))

        def load_wm(b):
            src = wm[b * PASS : (b + 1) * PASS, :].rearrange("(u t e) c -> t u e c", t=PACK, e=PACK)
            for t in range(PACK):
                nc.sync.dma_start(raws[4 + b][:, t, :], src[t])

        def cast(i):
            rounded[i] = placed("rounded%d" % i, [P, WIDE], BF16, at_rounded[i])
            if i < 4:
                nc.vector.tensor_copy(
                    out=rounded[i][:].rearrange("p (t u e j) -> p t u j e", t=PACK, e=PACK, j=PACK),
                    in_=raws[i][:].rearrange("p j (u t e) -> p t u j e", t=PACK, e=PACK),
                )
            else:
                nc.vector.tensor_copy(
                    out=rounded[i][:].rearrange("p (c i j) -> p c j i", i=4, j=PACK),
                    in_=raws[i][:].rearrange("p j (c i) -> p c j i", i=4),
                )

        def cast_wm_pool(i):
            rounded[i] = placed("rounded%d" % i, [P, WIDE], BF16, at_rounded[i])
            nc.gpsimd.tensor_scalar(
                out=rounded[i][:, 0 : POOL_CAST * PACK].rearrange("p (c j) -> p c j", j=PACK),
                in0=raws[i][:, :, 0:POOL_CAST].rearrange("p j c -> p c j"),
                scalar1=1.0,
                scalar2=0.0,
                op0=MULT,
                op1=ADD,
            )

        def cast_wm_rest(i):
            nc.vector.tensor_copy(
                out=rounded[i][:, POOL_CAST * PACK :].rearrange("p (c i j) -> p c j i", i=4, j=PACK),
                in_=raws[i][:, :, POOL_CAST:].rearrange("p j (c i) -> p c j i", i=4),
            )

        def quant_w(i):
            codes = keep.tile([P, PASS], U32, name="wcodes%d" % i, align_bytes=EDGE)
            scales = keep.tile([P, PASS], U8, name="wscales%d" % i, align_bytes=EDGE)
            nc.vector.quantize_mx(out=codes[:].bitcast(FP8X4), scales=scales[:], in_=rounded[i][:])
            quantised[i] = (codes, scales)

        ys = [keep.tile([P, WIDE], F32, name="y%d" % q) for q in range(4)]
        roots = [placed("root0", [P, WIDE], F32, at_root0)]
        roots = roots + [keep.tile([P, WIDE], F32, name="root%d" % q) for q in range(1, 3)]
        roots = roots + [placed("root3", [P, WIDE], F32, at_root3)]
        pool_gates = {q: placed("gate%d" % q, [P, WIDE], F32, at_gate[q]) for q in (1, 3)}

        third_gates = [placed("gate2%d" % g, [P, WIDE], F32, 64 * KB + g * (8 * KB - EDGE)) for g in range(2)]

        def gate(q, c):
            if q == 2:
                return third_gates[c // 2]
            return pool_gates[q] if q == 1 or (q == 3 and c >= 2) else ys[q]

        xs = {}
        fs = {}

        def project(q, t, passes, c0=0, c1=4, first_bank=0):
            h, b = divmod(q, 2)
            if (q, t, c0) not in xs:
                xs[q, t, c0] = bank(first_bank + t, [P, (c1 - c0) * CHUNK])
            for a in passes:
                nc.tensor.matmul_mx(
                    out=xs[q, t, c0][:],
                    lhsT=wkp[b][:, a, t * P // 2 : (t + 1) * P // 2].bitcast(U8).bitcast(FP4X4),
                    lhsT_scale=wk_scale(a, b, t),
                    rhs=tokens(a, h, c0, c1),
                    rhs_scale=token_scales(a, h, c0, c1),
                    start=(a == 0),
                    stop=(a == 1),
                )

        def chunks(q, tile, c0, c1):
            if q == 1:
                return tile[:].rearrange("p (t j) -> p t j", t=PACK)[:, :, c0 * CHUNK : c1 * CHUNK]
            pair = tile[:].rearrange("p (g t j) -> p g t j", g=2, t=PACK)[:, c0 // 2]
            return pair[:, :, (c0 % 2) * CHUNK : (c0 % 2 + c1 - c0) * CHUNK]

        def square(q, t, c0=0, c1=4):
            src = xs[q, t, c0][:]
            if q == 1 or c1 - c0 == 2:
                dst = chunks(q, ys[q], c0, c1)[:, t, :]
            else:
                dst = ys[q][:].rearrange("p (g t j) -> p g t j", g=2, t=PACK)[:, :, t, :]
                src = src.rearrange("p (g j) -> p g j", g=2)
            nc.scalar.activation(out=dst, in_=src, func=ACT.Square, bias=bias[:, q % 2, PACK * t : PACK * t + 1])
            if q <= 1 and c1 == 4:
                project(q + 1, t, (0, 1))

        def root(q, view):
            nc.scalar.activation(out=view(roots[q]), in_=view(ys[q]), func=ACT.Abs_reciprocal_sqrt, bias=1.0)

        def unroot(q, view, eng, c=0):
            if eng is nc.scalar:
                nc.scalar.activation(out=view(gate(q, c)), in_=view(roots[q]), func=ACT.Square)
            else:
                eng.tensor_tensor(out=view(gate(q, c)), in0=view(roots[q]), in1=view(roots[q]), op=MULT)

        def of_chunk(c):
            return lambda tile: chunks(0, tile, c, c + 1)

        def of_columns(lo, hi):
            return lambda tile: tile[:, lo:hi]

        def feature(q, c, i, passes=(0, 1)):
            h, b = divmod(q, 2)
            if (q, c) not in fs:
                fs[q, c] = bank(i, [P, PACK, CHUNK])
            for a in passes:
                codes, scales = quantised[2 * b + a]
                for t in range(PACK):
                    nc.tensor.matmul_mx(
                        out=fs[q, c][:, t, :],
                        lhsT=codes[:, t * P : (t + 1) * P].bitcast(FP8X4),
                        lhsT_scale=scales[:, t * P : (t + 1) * P],
                        rhs=tokens(a, h, c, c + 1),
                        rhs_scale=token_scales(a, h, c, c + 1),
                        start=(a == 0 and t == 0),
                        stop=(a == 1 and t == PACK - 1),
                    )

        slot_of = {}
        for c in range(4):
            slot_of[0, c] = c
            slot_of[1, c] = 4 + c
        for b in range(2):
            for c in range(2):
                slot_of[2 + b, c] = 8 + 2 * b + c
                slot_of[2 + b, 2 + c] = 12 + 2 * c + b
        hb = {}
        hcodes = [
            placed("hcodes2", [P, HALF], U32, at_root3) if q == 2 else keep.tile([P, HALF], U32, name="hcodes%d" % q, align_bytes=EDGE)
            for q in range(4)
        ]

        def h_codes(s0, s1):
            return hcodes[s0 // 4][:, (s0 % 4) * CHUNK : (s0 % 4 + s1 - s0) * CHUNK].bitcast(FP8X4)

        hscales = keep.tile([P, 16 * CHUNK], U8, name="hscales", align_bytes=EDGE)

        def h_slots(s0, s1):
            g = min(s0 // 4, 2)
            if g not in hb:
                hb[g] = placed("h%d" % g, [P, (1 + g // 2) * WIDE], BF16, at_h[g])
            return hb[g][:, (s0 - 4 * g) * PASS : (s1 - 4 * g) * PASS]

        def weigh(q, c):
            s0 = slot_of[q, c]
            nc.vector.tensor_tensor(
                out=h_slots(s0, s0 + 1).rearrange("p (u i t) -> p u t i", i=4, t=PACK),
                in0=fs[q, c][:].rearrange("p t (u i) -> p u t i", i=4),
                in1=chunks(q, gate(q, c), c, c + 1).rearrange("p t (u i) -> p u t i", i=4),
                op=MULT,
            )

        def quant_h(s0, s1):
            nc.vector.quantize_mx(
                out=h_codes(s0, s1),
                scales=hscales[:, s0 * CHUNK : s1 * CHUNK],
                in_=h_slots(s0, s1),
            )

        out_view = out.rearrange("(g p) s -> p g s", p=P)

        def piece(h, c0, c1, g0, g1, i):
            return bank(i, [P, g1 - g0, (c1 - c0) * CHUNK]), h, c0, c1, g0, g1

        def mix(part, b, opening=0):
            acc, h, c0, c1, g0, g1 = part
            codes, scales = quantised[4 + b]
            s0 = slot_of[2 * h + b, c0]
            cols = slice(s0 * CHUNK, (s0 + c1 - c0) * CHUNK)
            for g in range(g0, g1):
                nc.tensor.matmul_mx(
                    out=acc[:, g - g0, :],
                    lhsT=codes[:, g * P : (g + 1) * P].bitcast(FP8X4),
                    lhsT_scale=scales[:, g * P : (g + 1) * P],
                    rhs=h_codes(s0, s0 + c1 - c0),
                    rhs_scale=hscales[:, cols],
                    start=(b == opening and g == g0),
                    stop=(b != opening and g == g1 - 1),
                )

        def store(part, eng, queue=nc.sync):
            acc, h, c0, c1, g0, g1 = part
            res = opool.tile(list(acc.shape), F32, name="res", tag="res")
            if eng is nc.vector:
                nc.vector.tensor_copy(out=res[:], in_=acc[:])
            else:
                nc.scalar.copy(out=res[:], in_=acc[:])
            queue.dma_start(out_view[:, g0:g1, h * HALF + c0 * CHUNK : h * HALF + c1 * CHUNK], res[:])

        gather(0, 0, S)
        load_wk(1)
        load_wf(0)
        load_wf(1)
        move_scales(1, [(28, nc.gpsimd)] + [(row, nc.sync) for row in range(24, 0, -4)])
        load_wf(2)
        load_wf(3)
        gather(1, 0, HALF // 2)
        gather(1, HALF // 2, HALF)
        permute_wk(1)
        gather(1, HALF, S)

        for t in range(PACK):
            project(0, t, (0,), 0, 2, PACK)
        for t in range(PACK):
            project(0, t, (0,), 2, 4, 0)
        for t in range(PACK):
            project(0, t, (1,), 0, 2, PACK)
            square(0, t, 0, 2)
        for t in range(PACK):
            project(0, t, (1,), 2, 4, 0)

        front = of_columns(0, WIDE // 2)
        back = of_columns(WIDE // 2, WIDE)
        cast(0)
        load_wm(0)
        square(0, 0, 2, 4)
        root(0, front)
        unroot(0, front, nc.vector)
        quant_w(0)
        for c in range(4):
            feature(0, c, PACK + c, (0,))
        for t in range(1, PACK):
            square(0, t, 2, 4)
        cast(1)
        load_wm(1)
        square(1, 0)
        root(0, back)
        unroot(0, of_chunk(2), nc.vector)
        quant_w(1)
        for c in range(4):
            feature(0, c, PACK + c, (1,))
        unroot(0, of_chunk(3), nc.vector)

        pooled = of_columns(0, POOL_COLS)
        rest = of_columns(POOL_COLS, WIDE)

        def start_roots(q):
            square(q, 2)
            root(q, pooled)
            square(q, 3)

        def finish_gates(q):
            square(q + 1, 0)
            root(q, rest)
            square(q + 1, 1)
            unroot(q, rest, nc.scalar)

        square(1, 1)
        start_roots(1)
        unroot(1, pooled, nc.gpsimd)
        finish_gates(1)
        for c in range(4):
            weigh(0, c)
            project(3, c, (0, 1), first_bank=PACK)
        square(2, 2)
        square(2, 3)
        cast(2)
        quant_h(0, 2)
        quant_w(2)
        for c in range(4):
            feature(1, c, c, (0,))
        cast(3)
        quant_h(2, 4)
        quant_w(3)
        for c in range(4):
            feature(1, c, c, (1,))
        cast(4)

        cast_wm_pool(5)
        for t in range(PACK):
            square(3, t)
        root(2, front)
        root(3, of_columns(0, WIDE))
        unroot(2, front, nc.scalar)
        unroot(3, front, nc.scalar)
        root(2, back)
        early = [(2, 0), (2, 1), (3, 0), (3, 1)]
        late = [(3, 2), (2, 2), (3, 3), (2, 3)]
        for c in range(4):
            weigh(1, c)
            feature(early[c][0], early[c][1], c)
        quant_w(4)
        cast_wm_rest(5)
        quant_h(4, 8)
        quant_w(5)

        for c in (2, 3):
            unroot(3, of_chunk(c), nc.gpsimd, 2)
        first = [piece(0, 0, 4, g, g + 1, PACK + g) for g in range(4)]
        for part in first:
            mix(part, 0)
        for part in first:
            mix(part, 1)
        for i in range(4):
            weigh(early[i][0], early[i][1])
            feature(late[i][0], late[i][1], i)
        for part in first[:3]:
            store(part, nc.scalar)
        unroot(2, of_chunk(2), nc.scalar, 2)
        store(first[3], nc.scalar)
        unroot(2, of_chunk(3), nc.scalar, 3)
        weigh(3, 2)
        quant_h(8, 12)
        second = [piece(1, 0, 2, 2 * j, 2 * j + 2, PACK + j) for j in range(2)]
        for part in second:
            mix(part, 0)
            mix(part, 1)
        weigh(2, 2)
        weigh(3, 3)
        quant_h(12, 14)
        third = piece(1, 2, 3, 0, 4, 6)
        mix(third, 0)
        mix(third, 1)
        weigh(2, 3)
        quant_h(15, 16)
        last = [piece(1, 3, 4, 0, 2, 7), piece(1, 3, 4, 2, 4, 0)]
        for part in last:
            mix(part, 1, 1)
        quant_h(14, 15)
        for part in last:
            mix(part, 0, 1)
        for part in second:
            store(part, nc.scalar)
        store(third, nc.scalar)
        store(last[0], nc.scalar, nc.scalar)
        store(last[1], nc.vector)
